import numpy as np
import ml_dtypes


def mxq(x, axis, fmt="e4m3"):
    dtype, down = {"e4m3": (ml_dtypes.float8_e4m3fn, 7), "e5m2": (ml_dtypes.float8_e5m2, 14)}[fmt]
    v = np.moveaxis(np.asarray(x, np.float32).astype(ml_dtypes.bfloat16).astype(np.float64), axis, -1)
    blocks = v.reshape(v.shape[:-1] + (-1, 32))
    amax = np.abs(blocks).max(-1, keepdims=True)
    byte = np.maximum(np.where(amax > 0, np.frexp(amax)[1] - 1 + 127, 0) - down, 1)
    scale = np.exp2(byte - 127.0)
    codes = (blocks / scale).astype(np.float32).astype(dtype).astype(np.float64)
    return np.moveaxis((codes * scale).reshape(v.shape), -1, axis)


WIDE = False


def mx_kscale(k):
    if not WIDE:
        return np.ones(k)
    levels = np.array([10, -10, 5, -5, 0])
    if k % 512:
        return np.exp2(np.random.permutation(np.resize(levels, k // 32))).repeat(32)
    a = np.empty((k // 512, 16))
    for p in range(k // 512):
        a[p, :8] = np.random.permutation(np.resize(levels, 8))
        for g in range(8):
            far = levels[np.abs(levels - a[p, g]) >= 10]
            a[p, g + 8] = far[np.random.randint(len(far))]
    return np.exp2(a.ravel()).repeat(32)


BF16 = ml_dtypes.bfloat16


def bf(x):
    return np.asarray(x, np.float32).astype(BF16)


def f64(x):
    return np.asarray(x).astype(np.float64)

def planes(Y):
    n, m = Y.shape
    b = f64(bf(Y)).reshape(n // 32, 32, m)
    amax = np.abs(b).max(1)
    byte = np.clip(np.where(amax > 0, np.frexp(amax)[1] - 1 + 127 - 7, 1), 1, 254)
    codes = (b * np.exp2(127.0 - byte)[:, None, :]).reshape(n, m).astype(np.float32).astype(ml_dtypes.float8_e4m3fn).view(np.uint8)
    words = codes.reshape(n // 512, 128, 4, m).transpose(0, 1, 3, 2)
    return np.ascontiguousarray(words), np.ascontiguousarray(byte.astype(np.uint8).reshape(n // 512, 16, m))


N, D, V = 1024, 1024, 2048

LOSS_SCALE = 1024.0
TEACHER_TEMPERATURE = 2.0
Z_GRAD_COEF = 0.02


def setup_inputs():
    s, t = mx_kscale(D), mx_kscale(V)
    return {
        "h": bf(np.random.standard_normal((N, D))),
        "gamma": bf((1.0 + 0.1 * np.random.standard_normal(D)) * s),
        "e": bf(np.random.standard_normal((V, D)) / np.sqrt(D) * t[:, None] / s[None, :]),
        "a": bf((1.0 + 0.1 * np.random.standard_normal(V)) / t),
        "b": bf(0.4 * np.random.standard_normal(V)),
        "teacher": bf(np.random.standard_normal((N, V)) * 2.0),
        "w": bf(np.random.uniform(0.5, 1.5, N)),
    }


def row_logsumexp(x):
    m = np.max(x, axis=-1, keepdims=True)
    return np.log(np.sum(np.exp(x - m), axis=-1, keepdims=True)) + m


def row_softmax(x):
    ex = np.exp(x - np.max(x, axis=-1, keepdims=True))
    return ex / np.sum(ex, axis=-1, keepdims=True)


def core(h, gamma, e, a, b, teacher, w):
    h, gamma, e, a, b, teacher, w = f64(h), f64(gamma), f64(e), f64(a), f64(b), f64(teacher), f64(w)
    hg = h * gamma[None, :]
    u = mxq(hg, 1, "e4m3") @ mxq(e, 1, "e4m3").T
    logits = a[None, :] * u + b[None, :]
    lse = row_logsumexp(logits)
    p = np.exp(logits - lse)
    t = row_softmax(teacher / TEACHER_TEMPERATURE)
    g = LOSS_SCALE * w[:, None] * (p * (1.0 + Z_GRAD_COEF * lse) - t)
    ga = g * a[None, :]
    return gamma[None, :] * (mxq(ga, 1, "e4m3") @ mxq(e, 0, "e4m3"))


def reference(h, gamma, e, a, b, teacher, w):
    R_out = core(h, gamma, e, a, b, teacher, w)
    words, scales = planes(R_out.T)
    return R_out, words, scales

@@ -1,0 +1,417 @@
+from contextlib import ExitStack
+
+import concourse.mybir as mybir
+from concourse.masks import make_identity
+
+N, D, V = 1024, 1024, 2048
+FLOPS = 4 * N * D * V
+
+F32 = mybir.dt.float32
+BF16 = mybir.dt.bfloat16
+U32 = mybir.dt.uint32
+I32 = mybir.dt.int32
+U8 = mybir.dt.uint8
+FP8X4 = mybir.dt.float8_e4m3fn_x4
+ALU = mybir.AluOpType
+ACT = mybir.ActivationFunctionType
+AX = mybir.AxisListType
+
+
+PRO = [("sv",), ("le", 1, 0, 1,), ("eT", 1, 0, 0,), ("le", 0, 0, 2,), ("lh", 0, 0,), ("eT", 1, 1, 0,), ("e2i", 1, 0, "S",), ("e2i", 1, 1, "V",), ("eTe", 1, 0, 0, "V",), ("eT", 1, 1, 1,), ("hmul", 0, 0,), ("lh", 0, 1,), ("hT", 0, 0,), ("eTe", 1, 1, 0, "S",), ("eT", 1, 0, 1,), ("hTe", 0, 0,), ("eTe", 1, 0, 1, "S",), ("qe2", 1, 1,), ("hmul", 0, 1,), ("lh", 1, 0,), ("le", 0, 1, 2,), ("hT", 0, 1,), ("le", 2, 0, 1,), ("hTe", 0, 1,), ("eT", 0, 0, 0,), ("le", 3, 0, 1,), ("hmul", 1, 0,), ("qe2", 1, 0,), ("eTe", 1, 1, 1, "S",), ("eTe", 0, 0, 0, "S",), ("lh", 2, 0,), ("eT", 0, 1, 1,), ("e2i", 0, 1, "V",), ("eT", 0, 1, 0,), ("eT", 0, 0, 1,), ("eTe", 0, 1, 0, "S",), ("hT", 1, 0,), ("eT", 2, 1, 1,), ("eTe", 0, 0, 1, "S",), ("hTe", 1, 0,), ("eT", 2, 0, 0,), ("qe1", 1, 1,), ("qh", 0,), ("eT", 2, 1, 0,), ("eT", 2, 0, 1,), ("eTe", 0, 1, 1, "S",), ("qe2", 0, 1,), ("eTe", 2, 0, 0, "S",), ("eT", 3, 1, 0,), ("eTe", 2, 1, 0, "S",), ("lh", 1, 1,), ("eT", 3, 0, 0,), ("qe1", 1, 0,), ("eTe", 2, 0, 1, "S",), ("qe1", 0, 0,), ("MM", 0, 1,), ("e2i", 0, 0, "V",), ("hmul", 2, 0,), ("lt", 0, 1,), ("e2i", 2, 0, "V",), ("eT", 3, 0, 1,), ("eTe", 2, 1, 1, "S",), ("eTe", 3, 1, 0, "S",), ("lt", 0, 0,), ("hmul", 1, 1,), ("Mev", 0, 1,), ("qe1", 2, 1,), ("eTe", 3, 0, 0, "S",), ("qe1", 0, 1,), ("eT", 3, 1, 1,), ("hT", 1, 1,), ("qe1", 2, 0,), ("eTe", 3, 1, 1, "S",), ("qe1", 3, 1,), ("Xt", 0, 1, 1,), ("eTe", 3, 0, 1, "S",), ("qe1", 3, 0,), ("hT", 2, 0,), ("e2i", 2, 1, "V",), ("lh", 2, 1,), ("MM", 0, 0,), ("hTe", 1, 1,), ("Mev", 0, 0,), ("MM", 0, 2,), ("Mev", 0, 2,), ("MM", 0, 3,), ("qh", 1,), ("Mev", 0, 3,), ("fold1", 0, 0,), ("fold1", 0, 2,), ("MM", 1, 2,), ("Mev", 1, 2,), ("fold1", 0, 1,), ("fold1", 0, 3,), ("fold2", 0, 0,), ("MM", 1, 3,), ("Mev", 1, 3,), ("fold2", 0, 1,), ("qe2", 0, 0,), ("fold3", 0,), ("tmax", 0, 1,), ("MM", 1, 0,), ("maxT", 0,), ("hTe", 2, 0,), ("Xt", 0, 1, 2,), ("maxR", 0,), ("e2i", 3, 1, "V",), ("Mev", 1, 0,), ("MM", 1, 1,), ("Xe", 0, 1, 2,), ("Xe", 0, 1, 1,), ("fold1", 1, 3,), ("Xt", 0, 0, 2,), ("Mev", 1, 1,), ("Xe", 0, 0, 2,), ("lh", 3, 0,), ("Xt", 0, 1, 3,), ("Xe", 0, 1, 3,), ("Xt", 0, 0, 1,), ("Xt", 0, 1, 0,), ("e2i", 3, 0, "V",), ("Xe", 0, 0, 1,), ("Xt", 0, 0, 0,), ("Xe", 0, 1, 0,), ("fold1", 1, 0,), ("tmax", 0, 0,), ("arow",), ("hmul", 2, 1,), ("fold1", 1, 1,), ("fold1", 1, 2,), ("Xe", 0, 0, 0,), ("fold2", 1, 0,), ("Xt", 0, 0, 3,), ("hT", 2, 1,), ("Xe", 0, 0, 3,), ("ssum", 0,), ("fold2", 1, 1,), ("spow", 0,), ("qe2", 2, 1,), ("fold3", 1,), ("hTe", 2, 1,), ("texp", 0, 1,), ("qh", 2,), ("lh", 3, 1,), ("texp", 0, 0,), ("ch1", 0,), ("qe2", 3, 0,), ("ch2", 0, 0,), ("qe2", 2, 0,), ("lt", 1, 1,), ("ch2", 0, 1,), ("qe2", 3, 1,), ("maxT", 1,), ("srec", 0,), ("ch2", 0, 2,), ("tk2", 0,), ("ch3", 0,), ("maxR", 1,), ("tk3", 0,), ("lt", 1, 0,)]
+BODY = [("Xt", 1, 0, 1,), ("pT", -1, 1, 1,), ("Xt", 1, 0, 0,), ("Xe", 1, 0, 1,), ("MM", 2, 3,), ("Xe", 1, 0, 0,), ("Mev", 2, 3,), ("hmul", 3, 0,), ("Xt", 1, 1, 0,), ("yy", 0, 0,), ("qga", 0, 0, 0,), ("yy", 0, 1,), ("MM", 2, 0,), ("Xe", 1, 1, 0,), ("fold1", 2, 3,), ("pT", -1, 1, 0,), ("hT", 3, 0,), ("Xt", 1, 1, 1,), ("Xt", 1, 0, 3,), ("pTe", -1, 1, 1,), ("gg", 0, 0, 1,), ("Mev", 2, 0,), ("Xe", 1, 0, 3,), ("pTe", -1, 1, 0,), ("Xe", 1, 1, 1,), ("hTe", 3, 0,), ("MM", 2, 2,), ("Mev", 2, 2,), ("Xt", 1, 0, 2,), ("Xt", 1, 1, 2,), ("Xe", 1, 0, 2,), ("gT", 0, 0, 1,), ("gTe", 0, 0, 1,), ("gT", 0, 0, 0,), ("gTe", 0, 0, 0,), ("MM", 2, 1,), ("Xe", 1, 1, 2,), ("Xt", 1, 1, 3,), ("fold1", 2, 0,), ("Xe", 1, 1, 3,), ("gg", 0, 1, 1,), ("hmul", 3, 1,), ("Mev", 2, 1,), ("qga", 0, 0, 1,), ("tmax", 1, 1,), ("ssum", 1,), ("fold1", 2, 2,), ("gT", 0, 1, 0,), ("spow", 1,), ("gT", 0, 1, 1,), ("MM2", 0, 0, 0,), ("tmax", 1, 0,), ("gTe", 0, 1, 0,), ("hT", 3, 1,), ("MM2", 0, 0, 1,), ("oev", 0, 0, 0,), ("gTe", 0, 1, 1,), ("qga", 0, 1, 1,), ("pT", 0, 0, 0,), ("texp", 1, 1,), ("srec", 1,), ("ch1", 1,), ("fold1", 2, 1,), ("ch2", 1, 0,), ("oev", 0, 0, 1,), ("hTe", 3, 1,), ("ch2", 1, 1,), ("MM2", 0, 1, 1,), ("texp", 1, 0,), ("fold2", 2, 0,), ("fold2", 2, 1,), ("gg", 0, 0, 0,), ("pT", 0, 0, 1,), ("oev", 0, 1, 1,), ("ch2", 1, 2,), ("fold3", 2,), ("qp", -1, 1, 0,), ("ch3", 1,), ("qp", -1, 1, 1,), ("qh", 3,), ("tk2", 1,), ("gg", 0, 1, 0,), ("MM2", 0, 1, 0,), ("lt", 2, 1,), ("pTe", 0, 0, 0,), ("qp", 0, 0, 0,), ("maxT", 2,), ("maxR", 2,), ("tk3", 1,), ("qga", 0, 1, 0,), ("pTe", 0, 0, 1,), ("qp", 0, 0, 1,), ("oev", 0, 1, 0,), ("lt", 2, 0,)]
+LAST = [("yy", 3, 0,), ("pT", 2, 1, 0,), ("pT", 2, 1, 1,), ("gg", 3, 0, 1,), ("pTe", 2, 1, 1,), ("pTe", 2, 1, 0,), ("gT", 3, 0, 1,), ("yy", 3, 1,), ("gT", 3, 0, 0,), ("gTe", 3, 0, 1,), ("gTe", 3, 0, 0,), ("qga", 3, 0, 1,), ("gg", 3, 1, 0,), ("MM2", 3, 0, 0,), ("gT", 3, 1, 0,), ("gg", 3, 1, 1,), ("qga", 3, 0, 0,), ("gTe", 3, 1, 0,), ("oev", 3, 0, 0,), ("MM2", 3, 0, 1,), ("qga", 3, 1, 0,), ("gT", 3, 1, 1,), ("pT", 3, 0, 0,), ("qp", 2, 1, 0,), ("oev", 3, 0, 1,), ("MM2", 3, 1, 0,), ("gTe", 3, 1, 1,), ("qga", 3, 1, 1,), ("pTe", 3, 0, 0,), ("qp", 3, 0, 0,), ("MM2", 3, 1, 1,), ("oev", 3, 1, 0,), ("pT", 3, 0, 1,), ("pT", 3, 1, 0,), ("qp", 2, 1, 1,), ("pTe", 3, 0, 1,), ("oev", 3, 1, 1,), ("pTe", 3, 1, 0,), ("qp", 3, 0, 1,), ("pT", 3, 1, 1,), ("qp", 3, 1, 0,), ("gg", 3, 0, 0,), ("pTe", 3, 1, 1,), ("qp", 3, 1, 1,)]
+
+
+def tile_distillzlosslogitsbackward_x1_kernel(tc, h, gamma, e, a, b, teacher, w, out_0, out_1, out_2):
+    nc = tc.nc
+    ctx = ExitStack()
+    with ctx:
+        sb = ctx.enter_context(tc.tile_pool(name="sb", bufs=1))
+        ps = ctx.enter_context(tc.psum_pool(name="ps", bufs=2))
+
+        def new(shape, dtype, tag, bufs, name):
+            return sb.tile(shape, dtype, name=name, tag=tag, bufs=bufs, align_bytes=64)
+
+        def bank(shape, tag, dtype=F32):
+            bk = ps.tile(shape, dtype, name="bk", tag=tag, bufs=2)
+            return bk
+
+        ctx.enter_context(tc.manual_schedule())
+
+        warm = new([128, 1], F32, "warm", 1, "warm")
+        nc.vector.memset(warm[:], 0.0)
+        nc.scalar.activation(out=warm[:], in_=warm[:], func=ACT.Exp)
+        grow0 = new([128, 1024], BF16, "grow0", 1, "grow0")
+        nc.vector.memset(grow0[:], 0.0)
+        nc.scalar.dma_start(out=grow0[0:1, :], in_=gamma.rearrange("(o d) -> o d", o=1))
+        ones = new([128, 128], BF16, "ones", 1, "ones")
+        nc.vector.memset(ones[:], 1.0)
+        vec0 = new([128, 128], BF16, "vec0", 1, "vec0")
+        nc.vector.memset(vec0[:], 0.0)
+        nc.scalar.dma_start(out=vec0[0:16, :], in_=a.rearrange("(r c) -> r c", c=128))
+        nc.scalar.dma_start(out=vec0[16:32, :], in_=b.rearrange("(r c) -> r c", c=128))
+        nc.scalar.dma_start(out=vec0[32:40, :], in_=w.rearrange("(r c) -> r c", c=128))
+        root = new([128, 2], F32, "root", 1, "root")
+        nc.gpsimd.memset(root[:], 1.0 / 1024.0)
+        ident_f = new([128, 128], F32, "ident_f", 1, "ident_f")
+        make_identity(nc, ident_f[:])
+        ident_b = new([128, 128], BF16, "ident_b", 1, "ident_b")
+        make_identity(nc, ident_b[:])
+
+        h_sb, t_sb, e_sb = {}, {}, {}
+
+        def load_h(i):
+            h_sb[i] = new([128, 1024], BF16, "h", 3, "h_sb")
+            nc.sync.dma_start(out=h_sb[i][:], in_=h[128 * i:128 * (i + 1), :])
+
+        def load_t(i):
+            t_sb[i] = new([128, 2048], BF16, "t", 2, "t_sb")
+            nc.sync.dma_start(out=t_sb[i][:], in_=teacher[128 * i:128 * (i + 1), :])
+
+        def le(g, x, parts):
+            if g not in e_sb:
+                e_sb[g] = new([128, 4, 1024], BF16, "big", 7, "e_sb")
+            src = e[512 * g:512 * (g + 1), :].rearrange("(p j) d -> p j d", j=4)
+            wd = 1024 // parts
+            nc.sync.dma_start(out=e_sb[g][:, :, wd * x:wd * (x + 1)], in_=src[:, :, wd * x:wd * (x + 1)])
+
+        gamma_row = new([128, 1024], BF16, "gamma_row", 1, "gamma_row")
+        for x in range(2):
+            bk = bank([128, 512], "u")
+            nc.tensor.matmul(bk[:], lhsT=ones[:], rhs=grow0[:, 512 * x:512 * (x + 1)], start=True, stop=True)
+            nc.vector.tensor_copy(out=gamma_row[:, 512 * x:512 * (x + 1)], in_=bk[:])
+        a_row = new([128, 2048], BF16, "a_row", 1, "a_row")
+        cols = new([128, 40], F32, "cols", 1, "cols")
+        wcol = new([128, 8], F32, "wcol", 1, "wcol")
+
+        def small_vectors():
+            bkc = bank([128, 128], "l", BF16)
+            nc.tensor.transpose(bkc[:], vec0[:], ident_b[:])
+            nc.vector.tensor_copy(out=cols[:], in_=bkc[:, 0:40])
+            nc.vector.tensor_scalar(out=wcol[:], in0=cols[:, 32:40], scalar1=1024.0, scalar2=None, op0=ALU.mult)
+
+        def arow():
+            nc.sync.dma_start(out=a_row[:], in_=a.partition_broadcast(128))
+
+        e1c = new([128, 2, 2048], U32, "e1c", 1, "e1c")
+        e1s = new([128, 2, 2048], U8, "e1s", 1, "e1s")
+        e2c = new([128, 4, 1024], U32, "e2c", 1, "e2c")
+        e2s = new([128, 4, 1024], U8, "e2s", 1, "e2s")
+
+        def words_t(dst, words, base, ident):
+            for u in range(2):
+                nc.tensor.transpose(dst[:, u, :], words[:, base + u:base + 256:2], ident[:])
+
+        e1g = {}
+
+        ebk = {}
+
+        def eT(g, gd, J):
+            words = e_sb[g][:].rearrange("p j d -> p (j d)").bitcast(F32)
+            ebk[g, gd, J] = bank([128, 2, 2, 128], "tr" if J == 0 else ("o" if gd == 0 else "l"))
+            for k in range(2):
+                words_t(ebk[g, gd, J][:, k], words, 512 * (2 * J + k) + 256 * gd, ident_f)
+
+        def eTe(g, gd, J, en):
+            if (g, gd) not in e1g:
+                e1g[g, gd] = new([128, 512, 4], BF16, "b4", 9, "e1g")
+            gv = e1g[g, gd][:].rearrange("q v t -> q (v t)").bitcast(F32).rearrange("q (p J k u) -> q J p k u", J=2, k=2, u=2)
+            src = ebk[g, gd, J][:].rearrange("q k u p -> q p k u")
+            if en == "S":
+                nc.scalar.copy(out=gv[:, J], in_=src)
+            else:
+                nc.vector.tensor_copy(out=gv[:, J], in_=src)
+
+        def qe1(g, gd):
+            nc.vector.quantize_mx(
+                out=e1c[:, gd, 512 * g:512 * (g + 1)].bitcast(FP8X4),
+                scales=e1s[:, gd, 512 * g:512 * (g + 1)],
+                in_=e1g[g, gd][:].rearrange("q v t -> q (v t)"),
+            )
+
+        e2g = {}
+
+        def e2i(g, dh, en):
+            grp = new([128, 512, 4], BF16, "b4", 9, "e2g")
+            e2g[g, dh] = grp
+            src = e_sb[g][:, :, 512 * dh:512 * (dh + 1)]
+            if en == "S":
+                nc.scalar.copy(out=grp[:], in_=src.rearrange("p j d -> p d j"))
+            elif en == "V":
+                nc.vector.tensor_copy(out=grp[:].rearrange("p (c i) t -> p c t i", i=4), in_=src.rearrange("p t (c i) -> p c t i", i=4))
+            else:
+                for x in range(2):
+                    nc.gpsimd.tensor_scalar(out=grp[:, 256 * x:256 * (x + 1), :], in0=src[:, :, 256 * x:256 * (x + 1)].rearrange("p j d -> p d j"), scalar1=1.0, scalar2=0.0, op0=ALU.mult, op1=ALU.add)
+
+        def qe2(g, dh):
+            nc.vector.quantize_mx(
+                out=e2c[:, g, 512 * dh:512 * (dh + 1)].bitcast(FP8X4),
+                scales=e2s[:, g, 512 * dh:512 * (dh + 1)],
+                in_=e2g[g, dh][:].rearrange("q v t -> q (v t)"),
+            )
+
+        hg, hgT, hgc, hgs = {}, {}, {}, {}
+
+        def hmul(s, i):
+            hg[s, i] = new([128, 1024], BF16, "hg", 2, "hg")
+            nc.vector.tensor_tensor(out=hg[s, i][:], in0=h_sb[2 * s + i][:], in1=gamma_row[:], op=ALU.mult)
+
+        hbk = {}
+
+        def hT(s, i):
+            hbk[s, i] = bank([128, 2, 2, 128], "tr")
+            words = hg[s, i][:].bitcast(F32)
+            for gd in range(2):
+                words_t(hbk[s, i][:, gd], words, 256 * gd, ident_f)
+
+        def hTe(s, i):
+            if s not in hgT:
+                hgT[s] = new([128, 2, 256, 4], BF16, "b4", 9, "hgT")
+            dst = hgT[s][:].rearrange("q g n t -> q (g n t)").bitcast(F32).rearrange("q (g i n u) -> q i g n u", g=2, i=2, u=2)
+            nc.scalar.copy(out=dst[:, i], in_=hbk[s, i][:].rearrange("q g u n -> q g n u"))
+
+        def qh(s):
+            hgc[s] = new([128, 2, 256], U32, "hgc", 3, "hgc")
+            hgs[s] = new([128, 2, 256], U8, "hgs", 3, "hgs")
+            nc.vector.quantize_mx(
+                out=hgc[s][:].rearrange("q g n -> q (g n)").bitcast(FP8X4),
+                scales=hgs[s][:].rearrange("q g n -> q (g n)"),
+                in_=hgT[s][:].rearrange("q g n t -> q (g n t)"),
+            )
+
+        ub, lT = {}, {}
+
+        def MM(s, g):
+            for k2 in range(2):
+                bk = bank([128, 2, 256], "u")
+                ub[s, g, k2] = bk
+                for k in range(2):
+                    vt = 4 * g + 2 * k2 + k
+                    for gd in range(2):
+                        nc.tensor.matmul_mx(
+                            out=bk[:, k, :],
+                            lhsT=e1c[:, gd, 128 * vt:128 * (vt + 1)].bitcast(FP8X4),
+                            lhsT_scale=e1s[:, gd, 128 * vt:128 * (vt + 1)],
+                            rhs=hgc[s][:, gd, :].bitcast(FP8X4),
+                            rhs_scale=hgs[s][:, gd, :],
+                            start=(gd == 0),
+                            stop=(gd == 1),
+                        )
+
+        def Mev(s, g):
+            lT[s, g] = new([128, 4, 256], F32, "lT", 8, "lT")
+            for q in range(4):
+                vt = 4 * g + q
+                nc.scalar.activation(out=lT[s, g][:, q, :], in_=ub[s, g, q // 2][:, q % 2, :], func=ACT.Identity, bias=cols[:, 16 + vt:17 + vt], scale=cols[:, vt:vt + 1])
+
+        f1, f2, negm, mtp, f4s = {}, {}, {}, {}, {}
+
+        def fold1(s, g):
+            if (s, g // 2) not in f1:
+                f1[s, g // 2] = new([128, 2, 512], BF16, "f1", 2, "f1")
+            nc.vector.tensor_tensor(out=f1[s, g // 2][:, g % 2, :].rearrange("p (q n) -> p q n", q=2), in0=lT[s, g][:, 0:2, :], in1=lT[s, g][:, 2:4, :], op=ALU.max)
+
+        def fold2(s, k):
+            if s not in f2:
+                f2[s] = new([128, 2, 512], BF16, "f2", 2, "f2")
+            nc.vector.tensor_tensor(out=f2[s][:, k, :], in0=f1[s, k][:, 0, :], in1=f1[s, k][:, 1, :], op=ALU.max)
+
+        def fold3(s):
+            f3 = new([128, 512], BF16, "f3", 1, "f3")
+            nc.vector.tensor_tensor(out=f3[:], in0=f2[s][:, 0, :], in1=f2[s][:, 1, :], op=ALU.max)
+            f4 = new([128, 256], BF16, "f4", 2, "f4")
+            nc.vector.tensor_tensor(out=f4[:], in0=f3[:, 0:256], in1=f3[:, 256:512], op=ALU.max)
+            f4s[s] = f4
+
+        def maxT(s):
+            mtp[s] = bank([128, 2, 128], "tr", BF16)
+            for i in range(2):
+                nc.tensor.transpose(mtp[s][:, i, :], f4s[s][:, 128 * i:128 * (i + 1)], ident_b[:])
+
+        def maxR(s):
+            negm[s] = new([128, 2], F32, "negm", 2, "negm")
+            nc.vector.tensor_reduce(out=negm[s][:], in_=mtp[s][:], axis=AX.X, op=ALU.max, negate=True)
+
+        tmx, St, Et = {}, {}, {}
+
+        def tmax(s, i):
+            if s not in tmx:
+                tmx[s] = new([128, 2], F32, "tmx", 2, "tmx")
+            t = t_sb[2 * s + i]
+            nc.vector.tensor_scalar(out=t[:], in0=t[:], scalar1=-0.5, scalar2=None, op0=ALU.mult, op1=ALU.min, accum_out=tmx[s][:, i:i + 1])
+
+        def texp(s, i):
+            if s not in St:
+                St[s] = new([128, 2], F32, "St", 2, "St")
+            Et[s, i] = new([128, 2048], F32, "big", 7, "Et")
+            nc.scalar.activation(out=Et[s, i][:], in_=t_sb[2 * s + i][:], func=ACT.Exp, bias=tmx[s][:, i:i + 1], scale=-1.0, accum_out=St[s][:, i:i + 1])
+
+        E, S4, lb = {}, {}, {}
+
+        def Xt(s, i, g):
+            lb[s, i, g] = bank([128, 4, 128], "l")
+            for q in range(4):
+                nc.tensor.transpose(lb[s, i, g][:, q, :], lT[s, g][:, q, 128 * i:128 * (i + 1)], ident_f[:])
+
+        def Xe(s, i, g):
+            if (s, i) not in E:
+                E[s, i] = new([128, 2048], F32, "big", 7, "E")
+            if s not in S4:
+                S4[s] = new([128, 2, 4], F32, "S4", 2, "S4")
+            nc.scalar.activation(out=E[s, i][:, 512 * g:512 * (g + 1)], in_=lb[s, i, g][:].rearrange("p q v -> p (q v)"), func=ACT.Exp, bias=negm[s][:, i:i + 1], scale=1.0, accum_out=S4[s][:, i, g:g + 1])
+
+        def col(nm):
+            return new([128, 2], F32, nm, 2, nm)
+
+        Ss, rS, zz, dd, pp, cc, rst, k2c, q1, rf = {}, {}, {}, {}, {}, {}, {}, {}, {}, {}
+
+        def ssum(s):
+            Ss[s] = col("Ss")
+            nc.vector.tensor_reduce(out=Ss[s][:], in_=S4[s][:], axis=AX.X, op=ALU.add)
+
+        def spow(s):
+            zz[s] = col("zz")
+            nc.gpsimd.tensor_tensor(out=zz[s][:], in0=Ss[s][:], in1=root[:], op=ALU.pow)
+
+        def srec(s):
+            rS[s] = col("rS")
+            nc.vector.reciprocal(out=rS[s][:], in_=Ss[s][:])
+
+        def ch1(s):
+            dd[s] = col("dd")
+            nc.vector.tensor_scalar(out=dd[s][:], in0=zz[s][:], scalar1=1.0, scalar2=None, op0=ALU.subtract)
+            pp[s, 0] = col("pp0")
+            nc.vector.tensor_scalar(out=pp[s, 0][:], in0=zz[s][:], scalar1=1.0, scalar2=-0.25, op0=ALU.subtract, op1=ALU.mult)
+
+        def ch2(s, k):
+            pp[s, k + 1] = col("pp%d" % (k + 1))
+            nc.vector.scalar_tensor_tensor(out=pp[s, k + 1][:], in0=pp[s, k][:], scalar=(1.0 / 3.0, -0.5, 1.0)[k], in1=dd[s][:], op0=ALU.add, op1=ALU.mult)
+
+        def ch3(s):
+            cc[s] = col("cc")
+            nc.vector.scalar_tensor_tensor(out=cc[s][:], in0=pp[s, 3][:], scalar=1024.0, in1=negm[s][:], op0=ALU.mult, op1=ALU.subtract)
+
+        def tk2(s):
+            rst[s] = col("rst")
+            nc.vector.reciprocal(out=rst[s][:], in_=St[s][:])
+            q1[s] = col("q1")
+            nc.vector.scalar_tensor_tensor(out=q1[s][:], in0=St[s][:], scalar=0.02, in1=rS[s][:], op0=ALU.mult, op1=ALU.mult)
+
+        def tk3(s):
+            k2c[s] = col("k2c")
+            nc.vector.tensor_tensor(out=k2c[s][:], in0=rst[s][:], in1=wcol[:, 2 * s:2 * s + 2], op=ALU.mult)
+            rf[s] = col("rf")
+            nc.vector.scalar_tensor_tensor(out=rf[s][:], in0=cc[s][:], scalar=50.0, in1=q1[s][:], op0=ALU.add, op1=ALU.mult)
+
+        ga, gaT, gac, gas, gbk = {}, {}, {}, {}, {}
+
+        def yy(s, i):
+            nc.vector.scalar_tensor_tensor(out=E[s, i][:], in0=E[s, i][:], scalar=rf[s][:, i:i + 1], in1=Et[s, i][:], op0=ALU.mult, op1=ALU.subtract)
+
+        def gg(s, i, x):
+            if (s, i) not in ga:
+                ga[s, i] = new([128, 2048], BF16, "b4", 9, "ga")
+            if (s, i) == (3, 1):
+                cs = slice(1024 * x, 1024 * (x + 1))
+            elif x == 1:
+                cs = slice(0, 2048)
+            else:
+                return
+            nc.vector.scalar_tensor_tensor(out=ga[s, i][:, cs], in0=E[s, i][:, cs], scalar=k2c[s][:, i:i + 1], in1=a_row[:, cs], op0=ALU.mult, op1=ALU.mult)
+
+        def gT(s, i, G):
+            words = ga[s, i][:].bitcast(F32)
+            gbk[s, i, G] = bank([128, 2, 2, 128], "tr")
+            for g in range(2):
+                words_t(gbk[s, i, G][:, g], words, 256 * (2 * G + g), ident_f)
+
+        def gTe(s, i, G):
+            if (s, i) not in gaT:
+                gaT[s, i] = new([128, 4, 128, 4], BF16, "b4", 9, "gaT")
+            dst = gaT[s, i][:].rearrange("q g n t -> q (g n t)").bitcast(F32).rearrange("q (G g n u) -> q G g n u", G=2, g=2, u=2)
+            nc.scalar.copy(out=dst[:, G], in_=gbk[s, i, G][:].rearrange("q g u n -> q g n u"))
+
+        def qga(s, i, G):
+            if (s, i) not in gac:
+                gac[s, i] = new([128, 512], U32, "gac", 2, "gac")
+                gas[s, i] = new([128, 512], U8, "gas", 2, "gas")
+            if (s, i) == (3, 1):
+                g0, g1 = 2 * G, 2 * G + 2
+            elif G == 1:
+                g0, g1 = 0, 4
+            else:
+                return
+            nc.vector.quantize_mx(
+                out=gac[s, i][:, 128 * g0:128 * g1].bitcast(FP8X4),
+                scales=gas[s, i][:, 128 * g0:128 * g1],
+                in_=gaT[s, i][:, g0:g1].rearrange("q g n t -> q (g n t)"),
+            )
+
+        ob, osb = {}, {}
+
+        def MM2(s, i, x):
+            for dh in range(2) if (s, i) == (3, 1) else (x,):
+                if (s, i, dh) not in ob:
+                    ob[s, i, dh] = bank([128, 512], "o")
+                for g in range(2 * x, 2 * x + 2) if (s, i) == (3, 1) else range(4):
+                    nc.tensor.matmul_mx(
+                        out=ob[s, i, dh][:],
+                        lhsT=gac[s, i][:, 128 * g:128 * (g + 1)].bitcast(FP8X4),
+                        lhsT_scale=gas[s, i][:, 128 * g:128 * (g + 1)],
+                        rhs=e2c[:, g, 512 * dh:512 * (dh + 1)].bitcast(FP8X4),
+                        rhs_scale=e2s[:, g, 512 * dh:512 * (dh + 1)],
+                        start=(g == 0),
+                        stop=(g == 3),
+                    )
+
+        def oev(s, i, dh):
+            osb[s, i, dh] = new([128, 512], F32, "osb", 4, "osb")
+            nc.vector.tensor_tensor(out=osb[s, i, dh][:], in0=ob[s, i, dh][:], in1=gamma_row[:, 512 * dh:512 * (dh + 1)], op=ALU.mult)
+            n0 = 128 * (2 * s + i)
+            nc.sync.dma_start(out=out_0[n0:n0 + 128, 512 * dh:512 * (dh + 1)], in_=osb[s, i, dh][:])
+
+        plg, plc, pls, pbk = {}, {}, {}, {}
+
+        def pT(s, i, dh):
+            pbk[s, i, dh] = bank([128, 4, 128], "tr")
+            for t in range(4):
+                nc.tensor.transpose(pbk[s, i, dh][:, t, :], osb[s, i, dh][:, t:512:4], ident_f[:])
+
+        def pTe(s, i, dh):
+            if (s, i) not in plg:
+                plg[s, i] = new([128, 2, 128, 4], BF16, "plg", 2, "plg")
+            nc.scalar.copy(out=plg[s, i][:, dh], in_=pbk[s, i, dh][:].rearrange("q t n -> q n t"))
+
+        o1 = out_1.bitcast(I32).rearrange("g p m o -> p g (m o)")
+        o2 = out_2.bitcast(I32).rearrange("g q m -> q g m")
+
+        def qp(s, i, dh):
+            if s not in pls:
+                pls[s] = new([128, 2, 256], U8, "pls", 2, "pls")
+            if (s, i) not in plc:
+                plc[s, i] = new([128, 2, 128], U32, "plc", 3, "plc")
+            nc.vector.quantize_mx(
+                out=plc[s, i][:, dh, :].bitcast(FP8X4),
+                scales=pls[s][:, dh, 128 * i:128 * (i + 1)],
+                in_=plg[s, i][:, dh].rearrange("q n t -> q (n t)"),
+            )
+            n0 = 128 * (2 * s + i)
+            if dh == 1:
+                nc.sync.dma_start(out=o1[:, :, n0:n0 + 128], in_=plc[s, i][:].bitcast(I32))
+            if i == 1 and dh == 1:
+                sv = pls[s][:].bitcast(I32)
+                for Q in range(4):
+                    nc.sync.dma_start(out=o2[4 * Q:4 * Q + 4, :, 64 * s:64 * (s + 1)], in_=sv[32 * Q:32 * Q + 4, :, :])
+
+
+        fns = dict(hmul=hmul, hT=hT, hTe=hTe, qh=qh, eT=eT, eTe=eTe, qe1=qe1, e2i=e2i, qe2=qe2, MM=MM, Mev=Mev, fold1=fold1, fold2=fold2, fold3=fold3, maxT=maxT, maxR=maxR,
+                   tmax=tmax, texp=texp, tk2=tk2, tk3=tk3, Xt=Xt, Xe=Xe, ssum=ssum, srec=srec, spow=spow, ch1=ch1, ch2=ch2, ch3=ch3, yy=yy, gg=gg, gT=gT, gTe=gTe, qga=qga,
+                   MM2=MM2, oev=oev, pT=pT, pTe=pTe, qp=qp, sv=small_vectors, arow=arow, le=le, lh=lambda s, i: load_h(2 * s + i), lt=lambda s, i: load_t(2 * s + i))
+        for it in PRO:
+            fns[it[0]](*it[1:])
+        for s in range(3):
+            for it in BODY:
+                if 0 <= s + it[1] < 4:
+                    fns[it[0]](s + it[1], *it[2:])
+        for it in LAST:
+            fns[it[0]](*it[1:])

@@ -16,402 +16,468 @@ ALU = mybir.AluOpType
 ACT = mybir.ActivationFunctionType
 AX = mybir.AxisListType
 
+LOSS_SCALE = 1024.0
+Z_COEF = 0.02
+ROOT = 1024.0
 
-PRO = [("sv",), ("le", 1, 0, 1,), ("eT", 1, 0, 0,), ("le", 0, 0, 2,), ("lh", 0, 0,), ("eT", 1, 1, 0,), ("e2i", 1, 0, "S",), ("e2i", 1, 1, "V",), ("eTe", 1, 0, 0, "V",), ("eT", 1, 1, 1,), ("hmul", 0, 0,), ("lh", 0, 1,), ("hT", 0, 0,), ("eTe", 1, 1, 0, "S",), ("eT", 1, 0, 1,), ("hTe", 0, 0,), ("eTe", 1, 0, 1, "S",), ("qe2", 1, 1,), ("hmul", 0, 1,), ("lh", 1, 0,), ("le", 0, 1, 2,), ("hT", 0, 1,), ("le", 2, 0, 1,), ("hTe", 0, 1,), ("eT", 0, 0, 0,), ("le", 3, 0, 1,), ("hmul", 1, 0,), ("qe2", 1, 0,), ("eTe", 1, 1, 1, "S",), ("eTe", 0, 0, 0, "S",), ("lh", 2, 0,), ("eT", 0, 1, 1,), ("e2i", 0, 1, "V",), ("eT", 0, 1, 0,), ("eT", 0, 0, 1,), ("eTe", 0, 1, 0, "S",), ("hT", 1, 0,), ("eT", 2, 1, 1,), ("eTe", 0, 0, 1, "S",), ("hTe", 1, 0,), ("eT", 2, 0, 0,), ("qe1", 1, 1,), ("qh", 0,), ("eT", 2, 1, 0,), ("eT", 2, 0, 1,), ("eTe", 0, 1, 1, "S",), ("qe2", 0, 1,), ("eTe", 2, 0, 0, "S",), ("eT", 3, 1, 0,), ("eTe", 2, 1, 0, "S",), ("lh", 1, 1,), ("eT", 3, 0, 0,), ("qe1", 1, 0,), ("eTe", 2, 0, 1, "S",), ("qe1", 0, 0,), ("MM", 0, 1,), ("e2i", 0, 0, "V",), ("hmul", 2, 0,), ("lt", 0, 1,), ("e2i", 2, 0, "V",), ("eT", 3, 0, 1,), ("eTe", 2, 1, 1, "S",), ("eTe", 3, 1, 0, "S",), ("lt", 0, 0,), ("hmul", 1, 1,), ("Mev", 0, 1,), ("qe1", 2, 1,), ("eTe", 3, 0, 0, "S",), ("qe1", 0, 1,), ("eT", 3, 1, 1,), ("hT", 1, 1,), ("qe1", 2, 0,), ("eTe", 3, 1, 1, "S",), ("qe1", 3, 1,), ("Xt", 0, 1, 1,), ("eTe", 3, 0, 1, "S",), ("qe1", 3, 0,), ("hT", 2, 0,), ("e2i", 2, 1, "V",), ("lh", 2, 1,), ("MM", 0, 0,), ("hTe", 1, 1,), ("Mev", 0, 0,), ("MM", 0, 2,), ("Mev", 0, 2,), ("MM", 0, 3,), ("qh", 1,), ("Mev", 0, 3,), ("fold1", 0, 0,), ("fold1", 0, 2,), ("MM", 1, 2,), ("Mev", 1, 2,), ("fold1", 0, 1,), ("fold1", 0, 3,), ("fold2", 0, 0,), ("MM", 1, 3,), ("Mev", 1, 3,), ("fold2", 0, 1,), ("qe2", 0, 0,), ("fold3", 0,), ("tmax", 0, 1,), ("MM", 1, 0,), ("maxT", 0,), ("hTe", 2, 0,), ("Xt", 0, 1, 2,), ("maxR", 0,), ("e2i", 3, 1, "V",), ("Mev", 1, 0,), ("MM", 1, 1,), ("Xe", 0, 1, 2,), ("Xe", 0, 1, 1,), ("fold1", 1, 3,), ("Xt", 0, 0, 2,), ("Mev", 1, 1,), ("Xe", 0, 0, 2,), ("lh", 3, 0,), ("Xt", 0, 1, 3,), ("Xe", 0, 1, 3,), ("Xt", 0, 0, 1,), ("Xt", 0, 1, 0,), ("e2i", 3, 0, "V",), ("Xe", 0, 0, 1,), ("Xt", 0, 0, 0,), ("Xe", 0, 1, 0,), ("fold1", 1, 0,), ("tmax", 0, 0,), ("arow",), ("hmul", 2, 1,), ("fold1", 1, 1,), ("fold1", 1, 2,), ("Xe", 0, 0, 0,), ("fold2", 1, 0,), ("Xt", 0, 0, 3,), ("hT", 2, 1,), ("Xe", 0, 0, 3,), ("ssum", 0,), ("fold2", 1, 1,), ("spow", 0,), ("qe2", 2, 1,), ("fold3", 1,), ("hTe", 2, 1,), ("texp", 0, 1,), ("qh", 2,), ("lh", 3, 1,), ("texp", 0, 0,), ("ch1", 0,), ("qe2", 3, 0,), ("ch2", 0, 0,), ("qe2", 2, 0,), ("lt", 1, 1,), ("ch2", 0, 1,), ("qe2", 3, 1,), ("maxT", 1,), ("srec", 0,), ("ch2", 0, 2,), ("tk2", 0,), ("ch3", 0,), ("maxR", 1,), ("tk3", 0,), ("lt", 1, 0,)]
-BODY = [("Xt", 1, 0, 1,), ("pT", -1, 1, 1,), ("Xt", 1, 0, 0,), ("Xe", 1, 0, 1,), ("MM", 2, 3,), ("Xe", 1, 0, 0,), ("Mev", 2, 3,), ("hmul", 3, 0,), ("Xt", 1, 1, 0,), ("yy", 0, 0,), ("qga", 0, 0, 0,), ("yy", 0, 1,), ("MM", 2, 0,), ("Xe", 1, 1, 0,), ("fold1", 2, 3,), ("pT", -1, 1, 0,), ("hT", 3, 0,), ("Xt", 1, 1, 1,), ("Xt", 1, 0, 3,), ("pTe", -1, 1, 1,), ("gg", 0, 0, 1,), ("Mev", 2, 0,), ("Xe", 1, 0, 3,), ("pTe", -1, 1, 0,), ("Xe", 1, 1, 1,), ("hTe", 3, 0,), ("MM", 2, 2,), ("Mev", 2, 2,), ("Xt", 1, 0, 2,), ("Xt", 1, 1, 2,), ("Xe", 1, 0, 2,), ("gT", 0, 0, 1,), ("gTe", 0, 0, 1,), ("gT", 0, 0, 0,), ("gTe", 0, 0, 0,), ("MM", 2, 1,), ("Xe", 1, 1, 2,), ("Xt", 1, 1, 3,), ("fold1", 2, 0,), ("Xe", 1, 1, 3,), ("gg", 0, 1, 1,), ("hmul", 3, 1,), ("Mev", 2, 1,), ("qga", 0, 0, 1,), ("tmax", 1, 1,), ("ssum", 1,), ("fold1", 2, 2,), ("gT", 0, 1, 0,), ("spow", 1,), ("gT", 0, 1, 1,), ("MM2", 0, 0, 0,), ("tmax", 1, 0,), ("gTe", 0, 1, 0,), ("hT", 3, 1,), ("MM2", 0, 0, 1,), ("oev", 0, 0, 0,), ("gTe", 0, 1, 1,), ("qga", 0, 1, 1,), ("pT", 0, 0, 0,), ("texp", 1, 1,), ("srec", 1,), ("ch1", 1,), ("fold1", 2, 1,), ("ch2", 1, 0,), ("oev", 0, 0, 1,), ("hTe", 3, 1,), ("ch2", 1, 1,), ("MM2", 0, 1, 1,), ("texp", 1, 0,), ("fold2", 2, 0,), ("fold2", 2, 1,), ("gg", 0, 0, 0,), ("pT", 0, 0, 1,), ("oev", 0, 1, 1,), ("ch2", 1, 2,), ("fold3", 2,), ("qp", -1, 1, 0,), ("ch3", 1,), ("qp", -1, 1, 1,), ("qh", 3,), ("tk2", 1,), ("gg", 0, 1, 0,), ("MM2", 0, 1, 0,), ("lt", 2, 1,), ("pTe", 0, 0, 0,), ("qp", 0, 0, 0,), ("maxT", 2,), ("maxR", 2,), ("tk3", 1,), ("qga", 0, 1, 0,), ("pTe", 0, 0, 1,), ("qp", 0, 0, 1,), ("oev", 0, 1, 0,), ("lt", 2, 0,)]
-LAST = [("yy", 3, 0,), ("pT", 2, 1, 0,), ("pT", 2, 1, 1,), ("gg", 3, 0, 1,), ("pTe", 2, 1, 1,), ("pTe", 2, 1, 0,), ("gT", 3, 0, 1,), ("yy", 3, 1,), ("gT", 3, 0, 0,), ("gTe", 3, 0, 1,), ("gTe", 3, 0, 0,), ("qga", 3, 0, 1,), ("gg", 3, 1, 0,), ("MM2", 3, 0, 0,), ("gT", 3, 1, 0,), ("gg", 3, 1, 1,), ("qga", 3, 0, 0,), ("gTe", 3, 1, 0,), ("oev", 3, 0, 0,), ("MM2", 3, 0, 1,), ("qga", 3, 1, 0,), ("gT", 3, 1, 1,), ("pT", 3, 0, 0,), ("qp", 2, 1, 0,), ("oev", 3, 0, 1,), ("MM2", 3, 1, 0,), ("gTe", 3, 1, 1,), ("qga", 3, 1, 1,), ("pTe", 3, 0, 0,), ("qp", 3, 0, 0,), ("MM2", 3, 1, 1,), ("oev", 3, 1, 0,), ("pT", 3, 0, 1,), ("pT", 3, 1, 0,), ("qp", 2, 1, 1,), ("pTe", 3, 0, 1,), ("oev", 3, 1, 1,), ("pTe", 3, 1, 0,), ("qp", 3, 0, 1,), ("pT", 3, 1, 1,), ("qp", 3, 1, 0,), ("gg", 3, 0, 0,), ("pTe", 3, 1, 1,), ("qp", 3, 1, 1,)]
+FIRST = """
+load_e 1 0 1; load_e 0 0 2; load_h 0 0; load_h 0 1; columns; turn_e 1 0 0; interleave_e 1 0 S; interleave_e 1 1 V;
+turn_e 1 0 1; load_h 1 0; gain 0 0; copy_e 1 0 0 S; gain 0 1; turn_e 1 1 0; quant_e2 1 0; copy_e 1 0 1 V; load_e 0 1 2;
+turn_e 1 1 1; turn_h 0 0; copy_e 1 1 0 S; gain 1 0; load_h 1 1; load_e 2 0 1; quant_e1 1 0; turn_h 0 1; copy_h 0 0;
+copy_h 0 1; quant_e2 1 1; turn_e 0 0 0; turn_e 0 1 0; turn_e 0 0 1; copy_e 0 0 0 V; copy_e 1 1 1 S; interleave_e 0 1 S;
+load_e 3 0 1; copy_e 0 1 0 S; turn_e 0 1 1; turn_e 2 0 0; copy_e 2 0 0 S; gain 1 1; quant_e1 1 1; turn_e 2 0 1;
+turn_e 2 1 0; turn_h 1 0; copy_e 0 1 1 S; copy_e 2 1 0 S; quant_h 0; copy_e 0 0 1 V; copy_h 1 0; turn_e 2 1 1;
+turn_e 3 1 0; interleave_e 0 0 V; copy_e 2 1 1 S; turn_h 1 1; copy_e 2 0 1 S; interleave_e 3 1 V; quant_e1 0 0;
+logits_mm 0 1; quant_e1 0 1; copy_h 1 1; interleave_e 2 1 V; quant_h 1; copy_e 3 1 0 S; quant_e1 2 0; load_teacher 0 1;
+quant_e2 0 1; turn_e 3 1 1; turn_e 3 0 0; logits_out 0 1; copy_e 3 1 1 S; load_h 2 0; copy_e 3 0 0 S; logits_mm 0 0;
+load_h 2 1; turn_e 3 0 1; load_teacher 0 0; quant_e2 0 0; quant_e1 2 1; logits_out 0 0; logits_mm 0 2; logits_out 0 2;
+logits_mm 1 0; logits_out 1 0; interleave_e 2 0 V; copy_e 3 0 1 V; quant_e1 3 1; quant_e1 3 0; max_tiles 0 0;
+logits_mm 0 3; max_tiles 0 1; gain 2 0; logits_out 0 3; max_groups 0 0; max_tiles 0 2; logits_mm 1 3; max_tiles 0 3;
+max_groups 0 1; logits_out 1 3; max_last 0; max_tiles 1 0; logits_mm 1 2; turn_h 2 0; gain 2 1; logits_out 1 2;
+turn_max 0; logits_mm 1 1; turn_logits 0 1 3; copy_h 2 0; row_max 0; spread_a; logits_out 1 1; max_tiles 1 2;
+teacher_max 0 1; max_tiles 1 3; student_exp 0 1 3; turn_logits 0 1 0; student_exp 0 1 0; teacher_max 0 0; turn_h 2 1;
+turn_logits 0 1 2; turn_logits 0 1 1; student_exp 0 1 2; turn_logits 0 0 0; max_tiles 1 1; quant_e2 2 0;
+student_exp 0 1 1; max_groups 1 1; copy_h 2 1; student_exp 0 0 0; turn_logits 0 0 1; student_exp 0 0 1;
+interleave_e 3 0 V; turn_logits 0 0 3; student_exp 0 0 3; quant_e2 2 1; max_groups 1 0; turn_logits 0 0 2;
+student_exp 0 0 2; teacher_exp 0 0; sum_exp 0; load_h 3 0; load_h 3 1; quant_h 2; quant_e2 3 0; root_sum 0; inv_sum 0;
+quant_e2 3 1; max_last 1; log_first 0; turn_max 1; log_next 0 0; log_next 0 1; row_max 1; teacher_exp 0 1;
+log_next 0 2; ratio_sums 0; log_last 0; factors 0; load_teacher 1 1; load_teacher 1 0;
+"""
+
+STEP = """
+gain 3 0; gain 3 1; turn_logits 1 1 0; turn_logits 1 0 0; turn_out -1 1 1; logits_mm 2 3; turn_out -1 1 0;
+student_exp 1 1 0; diff 0 0; student_exp 1 0 0; turn_logits 1 1 3; turn_h 3 0; logits_out 2 3; copy_h 3 0; diff 0 1;
+copy_out -1 1 1; student_exp 1 1 3; turn_logits 1 0 3; logits_mm 2 0; grad 0 0 2; turn_logits 1 1 2; max_tiles 2 3;
+student_exp 1 0 3; logits_out 2 0; copy_out -1 1 0; turn_logits 1 0 1; student_exp 1 1 2; logits_mm 2 2;
+turn_logits 1 1 1; student_exp 1 0 1; turn_grad 0 0 0; grad 0 1 2; teacher_max 1 0; logits_out 2 2; turn_logits 1 0 2;
+copy_grad 0 0 0; max_tiles 2 0; turn_grad 0 0 1; max_tiles 2 2; copy_grad 0 0 1; student_exp 1 1 1; turn_h 3 1;
+copy_h 3 1; quant_grad 0 0 2; logits_mm 2 1; student_exp 1 0 2; logits_out 2 1; sum_exp 1; teacher_max 1 1;
+turn_grad 0 1 1; root_sum 1; turn_grad 0 1 0; copy_grad 0 1 1; copy_grad 0 1 0; max_groups 2 1; max_tiles 2 1;
+out_mm 0 0 0 2; teacher_exp 1 0; quant_out -1 1 0; out_mm 0 0 1 2; out_gain 0 0 0; teacher_exp 1 1; log_first 1;
+load_teacher 2 0; quant_grad 0 1 2; log_next 1 0; max_groups 2 0; inv_sum 1; load_teacher 2 1; turn_out 0 0 0;
+out_gain 0 0 1; quant_h 3; max_last 2; out_mm 0 1 0 2; log_next 1 1; out_mm 0 1 1 2; turn_out 0 0 1; quant_out -1 1 1;
+out_gain 0 1 0; copy_out 0 0 0; log_next 1 2; out_gain 0 1 1; log_last 1; ratio_sums 1; turn_max 2; row_max 2;
+copy_out 0 0 1; factors 1; quant_out 0 0 0; quant_out 0 0 1;
+"""
+
+LAST = """
+diff 3 0; grad 3 0 2; diff 3 1; turn_out 2 1 0; turn_grad 3 0 0; copy_out 2 1 0; turn_grad 3 0 1; copy_grad 3 0 0;
+grad 3 1 0; turn_out 2 1 1; copy_grad 3 0 1; quant_grad 3 0 2; grad 3 1 1; turn_grad 3 1 0; copy_out 2 1 1;
+copy_grad 3 1 0; quant_grad 3 1 0; out_mm 3 0 0 2; out_mm 3 0 1 2; out_gain 3 0 0; turn_grad 3 1 1; copy_grad 3 1 1;
+out_gain 3 0 1; quant_out 2 1 0; turn_out 3 0 0; copy_out 3 0 0; out_mm 3 1 2 0; quant_grad 3 1 1; out_mm 3 1 2 1;
+quant_out 2 1 1; out_gain 3 1 0; turn_out 3 0 1; copy_out 3 0 1; quant_out 3 0 0; out_gain 3 1 1; turn_out 3 1 0;
+copy_out 3 1 0; turn_out 3 1 1; copy_out 3 1 1; quant_out 3 0 1; quant_out 3 1 0; quant_out 3 1 1;
+"""
+
+
+def entries(table):
+    out = []
+    for entry in table.replace("\n", " ").split(";"):
+        parts = [x for x in entry.split(" ") if x != ""]
+        if len(parts) > 0:
+            out.append((parts[0], [x if x in ("S", "V") else int(x) for x in parts[1:]]))
+    return out
 
 
 def tile_distillzlosslogitsbackward_x1_kernel(tc, h, gamma, e, a, b, teacher, w, out_0, out_1, out_2):
     nc = tc.nc
-    ctx = ExitStack()
-    with ctx:
-        sb = ctx.enter_context(tc.tile_pool(name="sb", bufs=1))
-        ps = ctx.enter_context(tc.psum_pool(name="ps", bufs=2))
-
-        def new(shape, dtype, tag, bufs, name):
-            return sb.tile(shape, dtype, name=name, tag=tag, bufs=bufs, align_bytes=64)
-
-        def bank(shape, tag, dtype=F32):
-            bk = ps.tile(shape, dtype, name="bk", tag=tag, bufs=2)
-            return bk
-
+    with ExitStack() as ctx:
+        sbuf = ctx.enter_context(tc.tile_pool(name="sbuf", bufs=1))
+        psum = ctx.enter_context(tc.psum_pool(name="psum", bufs=2))
         ctx.enter_context(tc.manual_schedule())
 
-        warm = new([128, 1], F32, "warm", 1, "warm")
-        nc.vector.memset(warm[:], 0.0)
-        nc.scalar.activation(out=warm[:], in_=warm[:], func=ACT.Exp)
-        grow0 = new([128, 1024], BF16, "grow0", 1, "grow0")
-        nc.vector.memset(grow0[:], 0.0)
-        nc.scalar.dma_start(out=grow0[0:1, :], in_=gamma.rearrange("(o d) -> o d", o=1))
-        ones = new([128, 128], BF16, "ones", 1, "ones")
+        buffers = {
+            "h": 3,
+            "hg": 2,
+            "teacher": 2,
+            "8k": 7,
+            "4k": 9,
+            "hg codes": 3,
+            "logits": 8,
+            "ga codes": 2,
+            "out": 4,
+            "out4": 2,
+            "words": 3,
+            "scales": 2,
+        }
+
+        def new(shape, dtype, kind, name, bufs=1):
+            return sbuf.tile(shape, dtype, name=name, tag=kind, bufs=buffers.get(kind, bufs), align_bytes=64)
+
+        def small(name):
+            return new([128, 2], F32, name, name, 2)
+
+        def bank(shape, kind, dtype=F32):
+            return psum.tile(shape, dtype, name="bank", tag=kind, bufs=2)
+
+        first = new([128, 1], F32, "first", "first")
+        nc.vector.memset(first[:], 0.0)
+        nc.scalar.activation(out=first[:], in_=first[:], func=ACT.Exp)
+        gamma_in = new([128, D], BF16, "gamma_in", "gamma_in")
+        nc.vector.memset(gamma_in[:], 0.0)
+        nc.scalar.dma_start(out=gamma_in[0:1, :], in_=gamma.rearrange("(o d) -> o d", o=1))
+        ones = new([128, 128], BF16, "ones", "ones")
         nc.vector.memset(ones[:], 1.0)
-        vec0 = new([128, 128], BF16, "vec0", 1, "vec0")
-        nc.vector.memset(vec0[:], 0.0)
-        nc.scalar.dma_start(out=vec0[0:16, :], in_=a.rearrange("(r c) -> r c", c=128))
-        nc.scalar.dma_start(out=vec0[16:32, :], in_=b.rearrange("(r c) -> r c", c=128))
-        nc.scalar.dma_start(out=vec0[32:40, :], in_=w.rearrange("(r c) -> r c", c=128))
-        root = new([128, 2], F32, "root", 1, "root")
-        nc.gpsimd.memset(root[:], 1.0 / 1024.0)
-        ident_f = new([128, 128], F32, "ident_f", 1, "ident_f")
+        vec_in = new([128, 128], BF16, "vec_in", "vec_in")
+        nc.vector.memset(vec_in[:], 0.0)
+        nc.scalar.dma_start(out=vec_in[0:16, :], in_=a.rearrange("(r c) -> r c", c=128))
+        nc.scalar.dma_start(out=vec_in[16:32, :], in_=b.rearrange("(r c) -> r c", c=128))
+        nc.scalar.dma_start(out=vec_in[32:40, :], in_=w.rearrange("(r c) -> r c", c=128))
+        exponent = new([128, 2], F32, "exponent", "exponent")
+        nc.gpsimd.memset(exponent[:], 1.0 / ROOT)
+        ident_f = new([128, 128], F32, "ident_f", "ident_f")
         make_identity(nc, ident_f[:])
-        ident_b = new([128, 128], BF16, "ident_b", 1, "ident_b")
+        ident_b = new([128, 128], BF16, "ident_b", "ident_b")
         make_identity(nc, ident_b[:])
 
-        h_sb, t_sb, e_sb = {}, {}, {}
-
-        def load_h(i):
-            h_sb[i] = new([128, 1024], BF16, "h", 3, "h_sb")
-            nc.sync.dma_start(out=h_sb[i][:], in_=h[128 * i:128 * (i + 1), :])
-
-        def load_t(i):
-            t_sb[i] = new([128, 2048], BF16, "t", 2, "t_sb")
-            nc.sync.dma_start(out=t_sb[i][:], in_=teacher[128 * i:128 * (i + 1), :])
-
-        def le(g, x, parts):
-            if g not in e_sb:
-                e_sb[g] = new([128, 4, 1024], BF16, "big", 7, "e_sb")
-            src = e[512 * g:512 * (g + 1), :].rearrange("(p j) d -> p j d", j=4)
-            wd = 1024 // parts
-            nc.sync.dma_start(out=e_sb[g][:, :, wd * x:wd * (x + 1)], in_=src[:, :, wd * x:wd * (x + 1)])
-
-        gamma_row = new([128, 1024], BF16, "gamma_row", 1, "gamma_row")
+        gamma_row = new([128, D], BF16, "gamma_row", "gamma_row")
         for x in range(2):
-            bk = bank([128, 512], "u")
-            nc.tensor.matmul(bk[:], lhsT=ones[:], rhs=grow0[:, 512 * x:512 * (x + 1)], start=True, stop=True)
-            nc.vector.tensor_copy(out=gamma_row[:, 512 * x:512 * (x + 1)], in_=bk[:])
-        a_row = new([128, 2048], BF16, "a_row", 1, "a_row")
-        cols = new([128, 40], F32, "cols", 1, "cols")
-        wcol = new([128, 8], F32, "wcol", 1, "wcol")
+            spread = bank([128, 512], "u")
+            nc.tensor.matmul(spread[:], lhsT=ones[:], rhs=gamma_in[:, 512 * x : 512 * (x + 1)], start=True, stop=True)
+            nc.vector.tensor_copy(out=gamma_row[:, 512 * x : 512 * (x + 1)], in_=spread[:])
+        a_row = new([128, V], BF16, "a_row", "a_row")
+        cols = new([128, 40], F32, "cols", "cols")
+        w_cols = new([128, 8], F32, "w_cols", "w_cols")
 
-        def small_vectors():
-            bkc = bank([128, 128], "l", BF16)
-            nc.tensor.transpose(bkc[:], vec0[:], ident_b[:])
-            nc.vector.tensor_copy(out=cols[:], in_=bkc[:, 0:40])
-            nc.vector.tensor_scalar(out=wcol[:], in0=cols[:, 32:40], scalar1=1024.0, scalar2=None, op0=ALU.mult)
-
-        def arow():
+        def spread_a():
             nc.sync.dma_start(out=a_row[:], in_=a.partition_broadcast(128))
 
-        e1c = new([128, 2, 2048], U32, "e1c", 1, "e1c")
-        e1s = new([128, 2, 2048], U8, "e1s", 1, "e1s")
-        e2c = new([128, 4, 1024], U32, "e2c", 1, "e2c")
-        e2s = new([128, 4, 1024], U8, "e2s", 1, "e2s")
+        def columns():
+            turned = bank([128, 128], "logits", BF16)
+            nc.tensor.transpose(turned[:], vec_in[:], ident_b[:])
+            nc.vector.tensor_copy(out=cols[:], in_=turned[:, 0:40])
+            nc.vector.tensor_scalar(out=w_cols[:], in0=cols[:, 32:40], scalar1=LOSS_SCALE, scalar2=None, op0=ALU.mult)
 
-        def words_t(dst, words, base, ident):
+        h_in, t_in, e_in = {}, {}, {}
+
+        def load_h(s, i):
+            j = 2 * s + i
+            h_in[s, i] = new([128, D], BF16, "h", "h_in")
+            nc.sync.dma_start(out=h_in[s, i][:], in_=h[128 * j : 128 * (j + 1), :])
+
+        def load_teacher(s, i):
+            j = 2 * s + i
+            t_in[s, i] = new([128, V], BF16, "teacher", "t_in")
+            nc.sync.dma_start(out=t_in[s, i][:], in_=teacher[128 * j : 128 * (j + 1), :])
+
+        def load_e(g, x, parts):
+            if g not in e_in:
+                e_in[g] = new([128, 4, D], BF16, "8k", "e_in")
+            cs = slice(D // parts * x, D // parts * (x + 1))
+            nc.sync.dma_start(out=e_in[g][:, :, cs], in_=e[512 * g : 512 * (g + 1), :].rearrange("(p j) d -> p j d", j=4)[:, :, cs])
+
+        def turn_words(dst, words, base):
             for u in range(2):
-                nc.tensor.transpose(dst[:, u, :], words[:, base + u:base + 256:2], ident[:])
+                nc.tensor.transpose(dst[:, u, :], words[:, base + u : base + 256 : 2], ident_f[:])
 
-        e1g = {}
+        e1_codes = new([128, 2, V], U32, "e1_codes", "e1_codes")
+        e1_scales = new([128, 2, V], U8, "e1_scales", "e1_scales")
+        e_turned, e1_bf = {}, {}
 
-        ebk = {}
-
-        def eT(g, gd, J):
-            words = e_sb[g][:].rearrange("p j d -> p (j d)").bitcast(F32)
-            ebk[g, gd, J] = bank([128, 2, 2, 128], "tr" if J == 0 else ("o" if gd == 0 else "l"))
+        def turn_e(g, f, x):
+            words = e_in[g][:].rearrange("p j d -> p (j d)").bitcast(F32)
+            e_turned[g, f, x] = bank([128, 2, 2, 128], "turn" if x == 0 else ("out" if f == 0 else "logits"))
             for k in range(2):
-                words_t(ebk[g, gd, J][:, k], words, 512 * (2 * J + k) + 256 * gd, ident_f)
+                turn_words(e_turned[g, f, x][:, k], words, 512 * (2 * x + k) + 256 * f)
 
-        def eTe(g, gd, J, en):
-            if (g, gd) not in e1g:
-                e1g[g, gd] = new([128, 512, 4], BF16, "b4", 9, "e1g")
-            gv = e1g[g, gd][:].rearrange("q v t -> q (v t)").bitcast(F32).rearrange("q (p J k u) -> q J p k u", J=2, k=2, u=2)
-            src = ebk[g, gd, J][:].rearrange("q k u p -> q p k u")
-            if en == "S":
-                nc.scalar.copy(out=gv[:, J], in_=src)
+        def copy_e(g, f, x, engine):
+            if (g, f) not in e1_bf:
+                e1_bf[g, f] = new([128, 512, 4], BF16, "4k", "e1_bf")
+            dst = e1_bf[g, f][:].rearrange("q v t -> q (v t)").bitcast(F32).rearrange("q (p x k u) -> q x p k u", x=2, k=2, u=2)
+            src = e_turned[g, f, x][:].rearrange("q k u p -> q p k u")
+            if engine == "S":
+                nc.scalar.copy(out=dst[:, x], in_=src)
             else:
-                nc.vector.tensor_copy(out=gv[:, J], in_=src)
+                nc.vector.tensor_copy(out=dst[:, x], in_=src)
 
-        def qe1(g, gd):
+        def quant_e1(g, f):
             nc.vector.quantize_mx(
-                out=e1c[:, gd, 512 * g:512 * (g + 1)].bitcast(FP8X4),
-                scales=e1s[:, gd, 512 * g:512 * (g + 1)],
-                in_=e1g[g, gd][:].rearrange("q v t -> q (v t)"),
+                out=e1_codes[:, f, 512 * g : 512 * (g + 1)].bitcast(FP8X4),
+                scales=e1_scales[:, f, 512 * g : 512 * (g + 1)],
+                in_=e1_bf[g, f][:].rearrange("q v t -> q (v t)"),
             )
 
-        e2g = {}
+        e2_codes = new([128, 4, D], U32, "e2_codes", "e2_codes")
+        e2_scales = new([128, 4, D], U8, "e2_scales", "e2_scales")
+        e2_bf = {}
 
-        def e2i(g, dh, en):
-            grp = new([128, 512, 4], BF16, "b4", 9, "e2g")
-            e2g[g, dh] = grp
-            src = e_sb[g][:, :, 512 * dh:512 * (dh + 1)]
-            if en == "S":
-                nc.scalar.copy(out=grp[:], in_=src.rearrange("p j d -> p d j"))
-            elif en == "V":
-                nc.vector.tensor_copy(out=grp[:].rearrange("p (c i) t -> p c t i", i=4), in_=src.rearrange("p t (c i) -> p c t i", i=4))
+        def interleave_e(g, f, engine):
+            e2_bf[g, f] = new([128, 512, 4], BF16, "4k", "e2_bf")
+            src = e_in[g][:, :, 512 * f : 512 * (f + 1)]
+            if engine == "S":
+                nc.scalar.copy(out=e2_bf[g, f][:], in_=src.rearrange("p t c -> p c t"))
             else:
-                for x in range(2):
-                    nc.gpsimd.tensor_scalar(out=grp[:, 256 * x:256 * (x + 1), :], in0=src[:, :, 256 * x:256 * (x + 1)].rearrange("p j d -> p d j"), scalar1=1.0, scalar2=0.0, op0=ALU.mult, op1=ALU.add)
+                nc.vector.tensor_copy(out=e2_bf[g, f][:].rearrange("p (c i) t -> p c t i", i=4), in_=src.rearrange("p t (c i) -> p c t i", i=4))
 
-        def qe2(g, dh):
+        def quant_e2(g, f):
             nc.vector.quantize_mx(
-                out=e2c[:, g, 512 * dh:512 * (dh + 1)].bitcast(FP8X4),
-                scales=e2s[:, g, 512 * dh:512 * (dh + 1)],
-                in_=e2g[g, dh][:].rearrange("q v t -> q (v t)"),
+                out=e2_codes[:, g, 512 * f : 512 * (f + 1)].bitcast(FP8X4),
+                scales=e2_scales[:, g, 512 * f : 512 * (f + 1)],
+                in_=e2_bf[g, f][:].rearrange("p c t -> p (c t)"),
             )
 
-        hg, hgT, hgc, hgs = {}, {}, {}, {}
+        hg, hg_turned, hg_bf, hg_codes, hg_scales = {}, {}, {}, {}, {}
 
-        def hmul(s, i):
-            hg[s, i] = new([128, 1024], BF16, "hg", 2, "hg")
-            nc.vector.tensor_tensor(out=hg[s, i][:], in0=h_sb[2 * s + i][:], in1=gamma_row[:], op=ALU.mult)
+        def gain(s, i):
+            hg[s, i] = new([128, D], BF16, "hg", "hg")
+            nc.vector.tensor_tensor(out=hg[s, i][:], in0=h_in[s, i][:], in1=gamma_row[:], op=ALU.mult)
 
-        hbk = {}
+        def turn_h(s, i):
+            hg_turned[s, i] = bank([128, 2, 2, 128], "turn")
+            for f in range(2):
+                turn_words(hg_turned[s, i][:, f], hg[s, i][:].bitcast(F32), 256 * f)
 
-        def hT(s, i):
-            hbk[s, i] = bank([128, 2, 2, 128], "tr")
-            words = hg[s, i][:].bitcast(F32)
-            for gd in range(2):
-                words_t(hbk[s, i][:, gd], words, 256 * gd, ident_f)
+        def copy_h(s, i):
+            if s not in hg_bf:
+                hg_bf[s] = new([128, 2, 256, 4], BF16, "4k", "hg_bf")
+            dst = hg_bf[s][:].rearrange("q f n t -> q (f n t)").bitcast(F32).rearrange("q (f i n u) -> q i f n u", f=2, i=2, u=2)
+            nc.scalar.copy(out=dst[:, i], in_=hg_turned[s, i][:].rearrange("q f u n -> q f n u"))
 
-        def hTe(s, i):
-            if s not in hgT:
-                hgT[s] = new([128, 2, 256, 4], BF16, "b4", 9, "hgT")
-            dst = hgT[s][:].rearrange("q g n t -> q (g n t)").bitcast(F32).rearrange("q (g i n u) -> q i g n u", g=2, i=2, u=2)
-            nc.scalar.copy(out=dst[:, i], in_=hbk[s, i][:].rearrange("q g u n -> q g n u"))
-
-        def qh(s):
-            hgc[s] = new([128, 2, 256], U32, "hgc", 3, "hgc")
-            hgs[s] = new([128, 2, 256], U8, "hgs", 3, "hgs")
+        def quant_h(s):
+            hg_codes[s] = new([128, 2, 256], U32, "hg codes", "hg_codes")
+            hg_scales[s] = new([128, 2, 256], U8, "hg scales", "hg_scales", 3)
             nc.vector.quantize_mx(
-                out=hgc[s][:].rearrange("q g n -> q (g n)").bitcast(FP8X4),
-                scales=hgs[s][:].rearrange("q g n -> q (g n)"),
-                in_=hgT[s][:].rearrange("q g n t -> q (g n t)"),
+                out=hg_codes[s][:].rearrange("q f n -> q (f n)").bitcast(FP8X4),
+                scales=hg_scales[s][:].rearrange("q f n -> q (f n)"),
+                in_=hg_bf[s][:].rearrange("q f n t -> q (f n t)"),
             )
 
-        ub, lT = {}, {}
+        u_banks, logits = {}, {}
 
-        def MM(s, g):
-            for k2 in range(2):
-                bk = bank([128, 2, 256], "u")
-                ub[s, g, k2] = bk
-                for k in range(2):
-                    vt = 4 * g + 2 * k2 + k
-                    for gd in range(2):
-                        nc.tensor.matmul_mx(
-                            out=bk[:, k, :],
-                            lhsT=e1c[:, gd, 128 * vt:128 * (vt + 1)].bitcast(FP8X4),
-                            lhsT_scale=e1s[:, gd, 128 * vt:128 * (vt + 1)],
-                            rhs=hgc[s][:, gd, :].bitcast(FP8X4),
-                            rhs_scale=hgs[s][:, gd, :],
-                            start=(gd == 0),
-                            stop=(gd == 1),
-                        )
-
-        def Mev(s, g):
-            lT[s, g] = new([128, 4, 256], F32, "lT", 8, "lT")
-            for q in range(4):
-                vt = 4 * g + q
-                nc.scalar.activation(out=lT[s, g][:, q, :], in_=ub[s, g, q // 2][:, q % 2, :], func=ACT.Identity, bias=cols[:, 16 + vt:17 + vt], scale=cols[:, vt:vt + 1])
-
-        f1, f2, negm, mtp, f4s = {}, {}, {}, {}, {}
-
-        def fold1(s, g):
-            if (s, g // 2) not in f1:
-                f1[s, g // 2] = new([128, 2, 512], BF16, "f1", 2, "f1")
-            nc.vector.tensor_tensor(out=f1[s, g // 2][:, g % 2, :].rearrange("p (q n) -> p q n", q=2), in0=lT[s, g][:, 0:2, :], in1=lT[s, g][:, 2:4, :], op=ALU.max)
-
-        def fold2(s, k):
-            if s not in f2:
-                f2[s] = new([128, 2, 512], BF16, "f2", 2, "f2")
-            nc.vector.tensor_tensor(out=f2[s][:, k, :], in0=f1[s, k][:, 0, :], in1=f1[s, k][:, 1, :], op=ALU.max)
-
-        def fold3(s):
-            f3 = new([128, 512], BF16, "f3", 1, "f3")
-            nc.vector.tensor_tensor(out=f3[:], in0=f2[s][:, 0, :], in1=f2[s][:, 1, :], op=ALU.max)
-            f4 = new([128, 256], BF16, "f4", 2, "f4")
-            nc.vector.tensor_tensor(out=f4[:], in0=f3[:, 0:256], in1=f3[:, 256:512], op=ALU.max)
-            f4s[s] = f4
-
-        def maxT(s):
-            mtp[s] = bank([128, 2, 128], "tr", BF16)
-            for i in range(2):
-                nc.tensor.transpose(mtp[s][:, i, :], f4s[s][:, 128 * i:128 * (i + 1)], ident_b[:])
-
-        def maxR(s):
-            negm[s] = new([128, 2], F32, "negm", 2, "negm")
-            nc.vector.tensor_reduce(out=negm[s][:], in_=mtp[s][:], axis=AX.X, op=ALU.max, negate=True)
-
-        tmx, St, Et = {}, {}, {}
-
-        def tmax(s, i):
-            if s not in tmx:
-                tmx[s] = new([128, 2], F32, "tmx", 2, "tmx")
-            t = t_sb[2 * s + i]
-            nc.vector.tensor_scalar(out=t[:], in0=t[:], scalar1=-0.5, scalar2=None, op0=ALU.mult, op1=ALU.min, accum_out=tmx[s][:, i:i + 1])
-
-        def texp(s, i):
-            if s not in St:
-                St[s] = new([128, 2], F32, "St", 2, "St")
-            Et[s, i] = new([128, 2048], F32, "big", 7, "Et")
-            nc.scalar.activation(out=Et[s, i][:], in_=t_sb[2 * s + i][:], func=ACT.Exp, bias=tmx[s][:, i:i + 1], scale=-1.0, accum_out=St[s][:, i:i + 1])
-
-        E, S4, lb = {}, {}, {}
-
-        def Xt(s, i, g):
-            lb[s, i, g] = bank([128, 4, 128], "l")
-            for q in range(4):
-                nc.tensor.transpose(lb[s, i, g][:, q, :], lT[s, g][:, q, 128 * i:128 * (i + 1)], ident_f[:])
-
-        def Xe(s, i, g):
-            if (s, i) not in E:
-                E[s, i] = new([128, 2048], F32, "big", 7, "E")
-            if s not in S4:
-                S4[s] = new([128, 2, 4], F32, "S4", 2, "S4")
-            nc.scalar.activation(out=E[s, i][:, 512 * g:512 * (g + 1)], in_=lb[s, i, g][:].rearrange("p q v -> p (q v)"), func=ACT.Exp, bias=negm[s][:, i:i + 1], scale=1.0, accum_out=S4[s][:, i, g:g + 1])
-
-        def col(nm):
-            return new([128, 2], F32, nm, 2, nm)
-
-        Ss, rS, zz, dd, pp, cc, rst, k2c, q1, rf = {}, {}, {}, {}, {}, {}, {}, {}, {}, {}
-
-        def ssum(s):
-            Ss[s] = col("Ss")
-            nc.vector.tensor_reduce(out=Ss[s][:], in_=S4[s][:], axis=AX.X, op=ALU.add)
-
-        def spow(s):
-            zz[s] = col("zz")
-            nc.gpsimd.tensor_tensor(out=zz[s][:], in0=Ss[s][:], in1=root[:], op=ALU.pow)
-
-        def srec(s):
-            rS[s] = col("rS")
-            nc.vector.reciprocal(out=rS[s][:], in_=Ss[s][:])
-
-        def ch1(s):
-            dd[s] = col("dd")
-            nc.vector.tensor_scalar(out=dd[s][:], in0=zz[s][:], scalar1=1.0, scalar2=None, op0=ALU.subtract)
-            pp[s, 0] = col("pp0")
-            nc.vector.tensor_scalar(out=pp[s, 0][:], in0=zz[s][:], scalar1=1.0, scalar2=-0.25, op0=ALU.subtract, op1=ALU.mult)
-
-        def ch2(s, k):
-            pp[s, k + 1] = col("pp%d" % (k + 1))
-            nc.vector.scalar_tensor_tensor(out=pp[s, k + 1][:], in0=pp[s, k][:], scalar=(1.0 / 3.0, -0.5, 1.0)[k], in1=dd[s][:], op0=ALU.add, op1=ALU.mult)
-
-        def ch3(s):
-            cc[s] = col("cc")
-            nc.vector.scalar_tensor_tensor(out=cc[s][:], in0=pp[s, 3][:], scalar=1024.0, in1=negm[s][:], op0=ALU.mult, op1=ALU.subtract)
-
-        def tk2(s):
-            rst[s] = col("rst")
-            nc.vector.reciprocal(out=rst[s][:], in_=St[s][:])
-            q1[s] = col("q1")
-            nc.vector.scalar_tensor_tensor(out=q1[s][:], in0=St[s][:], scalar=0.02, in1=rS[s][:], op0=ALU.mult, op1=ALU.mult)
-
-        def tk3(s):
-            k2c[s] = col("k2c")
-            nc.vector.tensor_tensor(out=k2c[s][:], in0=rst[s][:], in1=wcol[:, 2 * s:2 * s + 2], op=ALU.mult)
-            rf[s] = col("rf")
-            nc.vector.scalar_tensor_tensor(out=rf[s][:], in0=cc[s][:], scalar=50.0, in1=q1[s][:], op0=ALU.add, op1=ALU.mult)
-
-        ga, gaT, gac, gas, gbk = {}, {}, {}, {}, {}
-
-        def yy(s, i):
-            nc.vector.scalar_tensor_tensor(out=E[s, i][:], in0=E[s, i][:], scalar=rf[s][:, i:i + 1], in1=Et[s, i][:], op0=ALU.mult, op1=ALU.subtract)
-
-        def gg(s, i, x):
-            if (s, i) not in ga:
-                ga[s, i] = new([128, 2048], BF16, "b4", 9, "ga")
-            if (s, i) == (3, 1):
-                cs = slice(1024 * x, 1024 * (x + 1))
-            elif x == 1:
-                cs = slice(0, 2048)
-            else:
-                return
-            nc.vector.scalar_tensor_tensor(out=ga[s, i][:, cs], in0=E[s, i][:, cs], scalar=k2c[s][:, i:i + 1], in1=a_row[:, cs], op0=ALU.mult, op1=ALU.mult)
-
-        def gT(s, i, G):
-            words = ga[s, i][:].bitcast(F32)
-            gbk[s, i, G] = bank([128, 2, 2, 128], "tr")
-            for g in range(2):
-                words_t(gbk[s, i, G][:, g], words, 256 * (2 * G + g), ident_f)
-
-        def gTe(s, i, G):
-            if (s, i) not in gaT:
-                gaT[s, i] = new([128, 4, 128, 4], BF16, "b4", 9, "gaT")
-            dst = gaT[s, i][:].rearrange("q g n t -> q (g n t)").bitcast(F32).rearrange("q (G g n u) -> q G g n u", G=2, g=2, u=2)
-            nc.scalar.copy(out=dst[:, G], in_=gbk[s, i, G][:].rearrange("q g u n -> q g n u"))
-
-        def qga(s, i, G):
-            if (s, i) not in gac:
-                gac[s, i] = new([128, 512], U32, "gac", 2, "gac")
-                gas[s, i] = new([128, 512], U8, "gas", 2, "gas")
-            if (s, i) == (3, 1):
-                g0, g1 = 2 * G, 2 * G + 2
-            elif G == 1:
-                g0, g1 = 0, 4
-            else:
-                return
-            nc.vector.quantize_mx(
-                out=gac[s, i][:, 128 * g0:128 * g1].bitcast(FP8X4),
-                scales=gas[s, i][:, 128 * g0:128 * g1],
-                in_=gaT[s, i][:, g0:g1].rearrange("q g n t -> q (g n t)"),
-            )
-
-        ob, osb = {}, {}
-
-        def MM2(s, i, x):
-            for dh in range(2) if (s, i) == (3, 1) else (x,):
-                if (s, i, dh) not in ob:
-                    ob[s, i, dh] = bank([128, 512], "o")
-                for g in range(2 * x, 2 * x + 2) if (s, i) == (3, 1) else range(4):
+        def logits_mm(s, g):
+            for k in range(4):
+                if k % 2 == 0:
+                    u_banks[s, g, k // 2] = bank([128, 2, 256], "u")
+                j = 4 * g + k
+                for f in range(2):
                     nc.tensor.matmul_mx(
-                        out=ob[s, i, dh][:],
-                        lhsT=gac[s, i][:, 128 * g:128 * (g + 1)].bitcast(FP8X4),
-                        lhsT_scale=gas[s, i][:, 128 * g:128 * (g + 1)],
-                        rhs=e2c[:, g, 512 * dh:512 * (dh + 1)].bitcast(FP8X4),
-                        rhs_scale=e2s[:, g, 512 * dh:512 * (dh + 1)],
+                        out=u_banks[s, g, k // 2][:, k % 2, :],
+                        lhsT=e1_codes[:, f, 128 * j : 128 * (j + 1)].bitcast(FP8X4),
+                        lhsT_scale=e1_scales[:, f, 128 * j : 128 * (j + 1)],
+                        rhs=hg_codes[s][:, f, :].bitcast(FP8X4),
+                        rhs_scale=hg_scales[s][:, f, :],
+                        start=(f == 0),
+                        stop=(f == 1),
+                    )
+
+        def logits_out(s, g):
+            logits[s, g] = new([128, 4, 256], F32, "logits", "logits")
+            for k in range(4):
+                j = 4 * g + k
+                nc.scalar.activation(out=logits[s, g][:, k, :], in_=u_banks[s, g, k // 2][:, k % 2, :], func=ACT.Identity, bias=cols[:, 16 + j : 17 + j], scale=cols[:, j : j + 1])
+
+        max_a, max_b, max_c, max_turned, neg_max = {}, {}, {}, {}, {}
+
+        def max_tiles(s, g):
+            if (s, g // 2) not in max_a:
+                max_a[s, g // 2] = new([128, 2, 512], BF16, "max_a", "max_a", 2)
+            nc.vector.tensor_tensor(out=max_a[s, g // 2][:, g % 2, :].rearrange("p (k n) -> p k n", k=2), in0=logits[s, g][:, 0:2, :], in1=logits[s, g][:, 2:4, :], op=ALU.max)
+
+        def max_groups(s, x):
+            if s not in max_b:
+                max_b[s] = new([128, 2, 512], BF16, "max_b", "max_b", 2)
+            nc.vector.tensor_tensor(out=max_b[s][:, x, :], in0=max_a[s, x][:, 0, :], in1=max_a[s, x][:, 1, :], op=ALU.max)
+
+        def max_last(s):
+            half = new([128, 512], BF16, "half", "half")
+            nc.vector.tensor_tensor(out=half[:], in0=max_b[s][:, 0, :], in1=max_b[s][:, 1, :], op=ALU.max)
+            max_c[s] = new([128, 256], BF16, "max_c", "max_c", 2)
+            nc.vector.tensor_tensor(out=max_c[s][:], in0=half[:, 0:256], in1=half[:, 256:512], op=ALU.max)
+
+        def turn_max(s):
+            max_turned[s] = bank([128, 2, 128], "turn", BF16)
+            for i in range(2):
+                nc.tensor.transpose(max_turned[s][:, i, :], max_c[s][:, 128 * i : 128 * (i + 1)], ident_b[:])
+
+        def row_max(s):
+            neg_max[s] = small("neg_max")
+            nc.vector.tensor_reduce(out=neg_max[s][:], in_=max_turned[s][:], axis=AX.X, op=ALU.max, negate=True)
+
+        t_shift, t_sum, t_exp = {}, {}, {}
+
+        def teacher_max(s, i):
+            if s not in t_shift:
+                t_shift[s] = small("t_shift")
+            t = t_in[s, i]
+            nc.vector.tensor_scalar(out=t[:], in0=t[:], scalar1=-0.5, scalar2=None, op0=ALU.mult, op1=ALU.min, accum_out=t_shift[s][:, i : i + 1])
+
+        def teacher_exp(s, i):
+            if s not in t_sum:
+                t_sum[s] = small("t_sum")
+            t_exp[s, i] = new([128, V], F32, "8k", "t_exp")
+            nc.scalar.activation(out=t_exp[s, i][:], in_=t_in[s, i][:], func=ACT.Exp, bias=t_shift[s][:, i : i + 1], scale=-1.0, accum_out=t_sum[s][:, i : i + 1])
+
+        turned, p_exp, part_sums = {}, {}, {}
+
+        def turn_logits(s, i, g):
+            turned[s, i, g] = bank([128, 4, 128], "logits")
+            for k in range(4):
+                nc.tensor.transpose(turned[s, i, g][:, k, :], logits[s, g][:, k, 128 * i : 128 * (i + 1)], ident_f[:])
+
+        def student_exp(s, i, g):
+            if (s, i) not in p_exp:
+                p_exp[s, i] = new([128, V], F32, "8k", "p_exp")
+            if s not in part_sums:
+                part_sums[s] = new([128, 2, 4], F32, "part_sums", "part_sums", 2)
+            nc.scalar.activation(
+                out=p_exp[s, i][:, 512 * g : 512 * (g + 1)],
+                in_=turned[s, i, g][:].rearrange("p k v -> p (k v)"),
+                func=ACT.Exp,
+                bias=neg_max[s][:, i : i + 1],
+                scale=1.0,
+                accum_out=part_sums[s][:, i, g : g + 1],
+            )
+
+        p_sum, p_inv, z, d_z, series, lse, t_inv, ratio, p_factor, row_factor = {}, {}, {}, {}, {}, {}, {}, {}, {}, {}
+
+        def sum_exp(s):
+            p_sum[s] = small("p_sum")
+            nc.vector.tensor_reduce(out=p_sum[s][:], in_=part_sums[s][:], axis=AX.X, op=ALU.add)
+
+        def root_sum(s):
+            z[s] = small("z")
+            nc.gpsimd.tensor_tensor(out=z[s][:], in0=p_sum[s][:], in1=exponent[:], op=ALU.pow)
+
+        def inv_sum(s):
+            p_inv[s] = small("p_inv")
+            nc.vector.reciprocal(out=p_inv[s][:], in_=p_sum[s][:])
+
+        def log_first(s):
+            d_z[s] = small("d_z")
+            nc.vector.tensor_scalar(out=d_z[s][:], in0=z[s][:], scalar1=1.0, scalar2=None, op0=ALU.subtract)
+            series[s, 0] = small("series0")
+            nc.vector.tensor_scalar(out=series[s, 0][:], in0=z[s][:], scalar1=1.0, scalar2=-0.25, op0=ALU.subtract, op1=ALU.mult)
+
+        def log_next(s, k):
+            series[s, k + 1] = small("series%d" % (k + 1))
+            nc.vector.scalar_tensor_tensor(out=series[s, k + 1][:], in0=series[s, k][:], scalar=(1.0 / 3.0, -0.5, 1.0)[k], in1=d_z[s][:], op0=ALU.add, op1=ALU.mult)
+
+        def log_last(s):
+            lse[s] = small("lse")
+            nc.vector.scalar_tensor_tensor(out=lse[s][:], in0=series[s, 3][:], scalar=ROOT, in1=neg_max[s][:], op0=ALU.mult, op1=ALU.subtract)
+
+        def ratio_sums(s):
+            t_inv[s] = small("t_inv")
+            nc.vector.reciprocal(out=t_inv[s][:], in_=t_sum[s][:])
+            ratio[s] = small("ratio")
+            nc.vector.scalar_tensor_tensor(out=ratio[s][:], in0=t_sum[s][:], scalar=Z_COEF, in1=p_inv[s][:], op0=ALU.mult, op1=ALU.mult)
+
+        def factors(s):
+            row_factor[s] = small("row_factor")
+            nc.vector.tensor_tensor(out=row_factor[s][:], in0=t_inv[s][:], in1=w_cols[:, 2 * s : 2 * s + 2], op=ALU.mult)
+            p_factor[s] = small("p_factor")
+            nc.vector.scalar_tensor_tensor(out=p_factor[s][:], in0=lse[s][:], scalar=1.0 / Z_COEF, in1=ratio[s][:], op0=ALU.add, op1=ALU.mult)
+
+        ga, ga_turned, ga_bf, ga_codes, ga_scales = {}, {}, {}, {}, {}
+
+        def halves(part):
+            return (0, 1) if part == 2 else (part,)
+
+        def groups(part):
+            return (0, 4) if part == 2 else (2 * part, 2 * part + 2)
+
+        def diff(s, i):
+            nc.vector.scalar_tensor_tensor(out=p_exp[s, i][:], in0=p_exp[s, i][:], scalar=p_factor[s][:, i : i + 1], in1=t_exp[s, i][:], op0=ALU.mult, op1=ALU.subtract)
+
+        def grad(s, i, part):
+            if (s, i) not in ga:
+                ga[s, i] = new([128, V], BF16, "4k", "ga")
+            g0, g1 = groups(part)
+            cs = slice(512 * g0, 512 * g1)
+            nc.vector.scalar_tensor_tensor(out=ga[s, i][:, cs], in0=p_exp[s, i][:, cs], scalar=row_factor[s][:, i : i + 1], in1=a_row[:, cs], op0=ALU.mult, op1=ALU.mult)
+
+        def turn_grad(s, i, x):
+            ga_turned[s, i, x] = bank([128, 2, 2, 128], "turn")
+            for k in range(2):
+                turn_words(ga_turned[s, i, x][:, k], ga[s, i][:].bitcast(F32), 256 * (2 * x + k))
+
+        def copy_grad(s, i, x):
+            if (s, i) not in ga_bf:
+                ga_bf[s, i] = new([128, 4, 128, 4], BF16, "4k", "ga_bf")
+            dst = ga_bf[s, i][:].rearrange("q g n t -> q (g n t)").bitcast(F32).rearrange("q (x k n u) -> q x k n u", x=2, k=2, u=2)
+            nc.scalar.copy(out=dst[:, x], in_=ga_turned[s, i, x][:].rearrange("q k u n -> q k n u"))
+
+        def quant_grad(s, i, part):
+            if (s, i) not in ga_codes:
+                ga_codes[s, i] = new([128, 512], U32, "ga codes", "ga_codes")
+                ga_scales[s, i] = new([128, 512], U8, "ga scales", "ga_scales", 2)
+            g0, g1 = groups(part)
+            nc.vector.quantize_mx(
+                out=ga_codes[s, i][:, 128 * g0 : 128 * g1].bitcast(FP8X4),
+                scales=ga_scales[s, i][:, 128 * g0 : 128 * g1],
+                in_=ga_bf[s, i][:, g0:g1].rearrange("q g n t -> q (g n t)"),
+            )
+
+        out_banks, out_sb, out_turned, out_bf, words_out, scales_out = {}, {}, {}, {}, {}, {}
+
+        def out_mm(s, i, f, part):
+            g0, g1 = groups(part)
+            for x in halves(f):
+                if (s, i, x) not in out_banks:
+                    out_banks[s, i, x] = bank([128, 512], "out")
+                for g in range(g0, g1):
+                    nc.tensor.matmul_mx(
+                        out=out_banks[s, i, x][:],
+                        lhsT=ga_codes[s, i][:, 128 * g : 128 * (g + 1)].bitcast(FP8X4),
+                        lhsT_scale=ga_scales[s, i][:, 128 * g : 128 * (g + 1)],
+                        rhs=e2_codes[:, g, 512 * x : 512 * (x + 1)].bitcast(FP8X4),
+                        rhs_scale=e2_scales[:, g, 512 * x : 512 * (x + 1)],
                         start=(g == 0),
                         stop=(g == 3),
                     )
 
-        def oev(s, i, dh):
-            osb[s, i, dh] = new([128, 512], F32, "osb", 4, "osb")
-            nc.vector.tensor_tensor(out=osb[s, i, dh][:], in0=ob[s, i, dh][:], in1=gamma_row[:, 512 * dh:512 * (dh + 1)], op=ALU.mult)
+        def out_gain(s, i, f):
+            out_sb[s, i, f] = new([128, 512], F32, "out", "out_sb")
+            nc.vector.tensor_tensor(out=out_sb[s, i, f][:], in0=out_banks[s, i, f][:], in1=gamma_row[:, 512 * f : 512 * (f + 1)], op=ALU.mult)
             n0 = 128 * (2 * s + i)
-            nc.sync.dma_start(out=out_0[n0:n0 + 128, 512 * dh:512 * (dh + 1)], in_=osb[s, i, dh][:])
+            nc.sync.dma_start(out=out_0[n0 : n0 + 128, 512 * f : 512 * (f + 1)], in_=out_sb[s, i, f][:])
 
-        plg, plc, pls, pbk = {}, {}, {}, {}
-
-        def pT(s, i, dh):
-            pbk[s, i, dh] = bank([128, 4, 128], "tr")
+        def turn_out(s, i, f):
+            out_turned[s, i, f] = bank([128, 4, 128], "turn")
             for t in range(4):
-                nc.tensor.transpose(pbk[s, i, dh][:, t, :], osb[s, i, dh][:, t:512:4], ident_f[:])
+                nc.tensor.transpose(out_turned[s, i, f][:, t, :], out_sb[s, i, f][:, t:512:4], ident_f[:])
 
-        def pTe(s, i, dh):
-            if (s, i) not in plg:
-                plg[s, i] = new([128, 2, 128, 4], BF16, "plg", 2, "plg")
-            nc.scalar.copy(out=plg[s, i][:, dh], in_=pbk[s, i, dh][:].rearrange("q t n -> q n t"))
+        def copy_out(s, i, f):
+            if (s, i) not in out_bf:
+                out_bf[s, i] = new([128, 2, 128, 4], BF16, "out4", "out_bf")
+            nc.scalar.copy(out=out_bf[s, i][:, f], in_=out_turned[s, i, f][:].rearrange("q t n -> q n t"))
 
-        o1 = out_1.bitcast(I32).rearrange("g p m o -> p g (m o)")
-        o2 = out_2.bitcast(I32).rearrange("g q m -> q g m")
+        words_hbm = out_1.bitcast(I32).rearrange("g p m o -> p g (m o)")
+        scales_hbm = out_2.bitcast(I32).rearrange("g q m -> q g m")
 
-        def qp(s, i, dh):
-            if s not in pls:
-                pls[s] = new([128, 2, 256], U8, "pls", 2, "pls")
-            if (s, i) not in plc:
-                plc[s, i] = new([128, 2, 128], U32, "plc", 3, "plc")
+        def quant_out(s, i, f):
+            if s not in scales_out:
+                scales_out[s] = new([128, 2, 256], U8, "scales", "scales_out")
+            if (s, i) not in words_out:
+                words_out[s, i] = new([128, 2, 128], U32, "words", "words_out")
             nc.vector.quantize_mx(
-                out=plc[s, i][:, dh, :].bitcast(FP8X4),
-                scales=pls[s][:, dh, 128 * i:128 * (i + 1)],
-                in_=plg[s, i][:, dh].rearrange("q n t -> q (n t)"),
+                out=words_out[s, i][:, f, :].bitcast(FP8X4),
+                scales=scales_out[s][:, f, 128 * i : 128 * (i + 1)],
+                in_=out_bf[s, i][:, f].rearrange("q n t -> q (n t)"),
             )
             n0 = 128 * (2 * s + i)
-            if dh == 1:
-                nc.sync.dma_start(out=o1[:, :, n0:n0 + 128], in_=plc[s, i][:].bitcast(I32))
-            if i == 1 and dh == 1:
-                sv = pls[s][:].bitcast(I32)
+            if f == 1:
+                nc.sync.dma_start(out=words_hbm[:, :, n0 : n0 + 128], in_=words_out[s, i][:].bitcast(I32))
+            if i == 1 and f == 1:
+                live = scales_out[s][:].bitcast(I32)
                 for Q in range(4):
-                    nc.sync.dma_start(out=o2[4 * Q:4 * Q + 4, :, 64 * s:64 * (s + 1)], in_=sv[32 * Q:32 * Q + 4, :, :])
+                    nc.sync.dma_start(out=scales_hbm[4 * Q : 4 * Q + 4, :, 64 * s : 64 * (s + 1)], in_=live[32 * Q : 32 * Q + 4, :, :])
 
-
-        fns = dict(hmul=hmul, hT=hT, hTe=hTe, qh=qh, eT=eT, eTe=eTe, qe1=qe1, e2i=e2i, qe2=qe2, MM=MM, Mev=Mev, fold1=fold1, fold2=fold2, fold3=fold3, maxT=maxT, maxR=maxR,
-                   tmax=tmax, texp=texp, tk2=tk2, tk3=tk3, Xt=Xt, Xe=Xe, ssum=ssum, srec=srec, spow=spow, ch1=ch1, ch2=ch2, ch3=ch3, yy=yy, gg=gg, gT=gT, gTe=gTe, qga=qga,
-                   MM2=MM2, oev=oev, pT=pT, pTe=pTe, qp=qp, sv=small_vectors, arow=arow, le=le, lh=lambda s, i: load_h(2 * s + i), lt=lambda s, i: load_t(2 * s + i))
-        for it in PRO:
-            fns[it[0]](*it[1:])
+        helpers = dict(
+            load_h=load_h, load_teacher=load_teacher, load_e=load_e, spread_a=spread_a, columns=columns,
+            turn_e=turn_e, copy_e=copy_e, quant_e1=quant_e1, interleave_e=interleave_e, quant_e2=quant_e2,
+            gain=gain, turn_h=turn_h, copy_h=copy_h, quant_h=quant_h, logits_mm=logits_mm, logits_out=logits_out,
+            max_tiles=max_tiles, max_groups=max_groups, max_last=max_last, turn_max=turn_max, row_max=row_max,
+            teacher_max=teacher_max, teacher_exp=teacher_exp, turn_logits=turn_logits, student_exp=student_exp,
+            sum_exp=sum_exp, root_sum=root_sum, inv_sum=inv_sum, log_first=log_first, log_next=log_next, log_last=log_last,
+            ratio_sums=ratio_sums, factors=factors, diff=diff, grad=grad, turn_grad=turn_grad, copy_grad=copy_grad,
+            quant_grad=quant_grad, out_mm=out_mm, out_gain=out_gain, turn_out=turn_out, copy_out=copy_out, quant_out=quant_out,
+        )
+        for name, args in entries(FIRST):
+            helpers[name](*args)
         for s in range(3):
-            for it in BODY:
-                if 0 <= s + it[1] < 4:
-                    fns[it[0]](s + it[1], *it[2:])
-        for it in LAST:
-            fns[it[0]](*it[1:])
+            for name, args in entries(STEP):
+                if 0 <= s + args[0] < 4:
+                    helpers[name](s + args[0], *args[1:])
+        for name, args in entries(LAST):
+            helpers[name](*args)

from contextlib import ExitStack

import concourse.mybir as mybir
from concourse.masks import make_identity

N, D, V = 1024, 1024, 2048
FLOPS = 4 * N * D * V

F32 = mybir.dt.float32
BF16 = mybir.dt.bfloat16
U32 = mybir.dt.uint32
I32 = mybir.dt.int32
U8 = mybir.dt.uint8
FP8X4 = mybir.dt.float8_e4m3fn_x4
ALU = mybir.AluOpType
ACT = mybir.ActivationFunctionType
AX = mybir.AxisListType

LOSS_SCALE = 1024.0
Z_COEF = 0.02
ROOT = 1024.0

FIRST = """
load_e 1 0 1; load_e 0 0 2; load_h 0 0; load_h 0 1; columns; turn_e 1 0 0; interleave_e 1 0 S; interleave_e 1 1 V;
turn_e 1 0 1; load_h 1 0; gain 0 0; copy_e 1 0 0 S; gain 0 1; turn_e 1 1 0; quant_e2 1 0; copy_e 1 0 1 V; load_e 0 1 2;
turn_e 1 1 1; turn_h 0 0; copy_e 1 1 0 S; gain 1 0; load_h 1 1; load_e 2 0 1; quant_e1 1 0; turn_h 0 1; copy_h 0 0;
copy_h 0 1; quant_e2 1 1; turn_e 0 0 0; turn_e 0 1 0; turn_e 0 0 1; copy_e 0 0 0 V; copy_e 1 1 1 S; interleave_e 0 1 S;
load_e 3 0 1; copy_e 0 1 0 S; turn_e 0 1 1; turn_e 2 0 0; copy_e 2 0 0 S; gain 1 1; quant_e1 1 1; turn_e 2 0 1;
turn_e 2 1 0; turn_h 1 0; copy_e 0 1 1 S; copy_e 2 1 0 S; quant_h 0; copy_e 0 0 1 V; copy_h 1 0; turn_e 2 1 1;
turn_e 3 1 0; interleave_e 0 0 V; copy_e 2 1 1 S; turn_h 1 1; copy_e 2 0 1 S; interleave_e 3 1 V; quant_e1 0 0;
logits_mm 0 1; quant_e1 0 1; copy_h 1 1; interleave_e 2 1 V; quant_h 1; copy_e 3 1 0 S; quant_e1 2 0; load_teacher 0 1;
quant_e2 0 1; turn_e 3 1 1; turn_e 3 0 0; logits_out 0 1; copy_e 3 1 1 S; load_h 2 0; copy_e 3 0 0 S; logits_mm 0 0;
load_h 2 1; turn_e 3 0 1; load_teacher 0 0; quant_e2 0 0; quant_e1 2 1; logits_out 0 0; logits_mm 0 2; logits_out 0 2;
logits_mm 1 0; logits_out 1 0; interleave_e 2 0 V; copy_e 3 0 1 V; quant_e1 3 1; quant_e1 3 0; max_tiles 0 0;
logits_mm 0 3; max_tiles 0 1; gain 2 0; logits_out 0 3; max_groups 0 0; max_tiles 0 2; logits_mm 1 3; max_tiles 0 3;
max_groups 0 1; logits_out 1 3; max_last 0; max_tiles 1 0; logits_mm 1 2; turn_h 2 0; gain 2 1; logits_out 1 2;
turn_max 0; logits_mm 1 1; turn_logits 0 1 3; copy_h 2 0; row_max 0; spread_a; logits_out 1 1; max_tiles 1 2;
teacher_max 0 1; max_tiles 1 3; student_exp 0 1 3; turn_logits 0 1 0; student_exp 0 1 0; teacher_max 0 0; turn_h 2 1;
turn_logits 0 1 2; turn_logits 0 1 1; student_exp 0 1 2; turn_logits 0 0 0; max_tiles 1 1; quant_e2 2 0;
student_exp 0 1 1; max_groups 1 1; copy_h 2 1; student_exp 0 0 0; turn_logits 0 0 1; student_exp 0 0 1;
interleave_e 3 0 V; turn_logits 0 0 3; student_exp 0 0 3; quant_e2 2 1; max_groups 1 0; turn_logits 0 0 2;
student_exp 0 0 2; teacher_exp 0 0; sum_exp 0; load_h 3 0; load_h 3 1; quant_h 2; quant_e2 3 0; root_sum 0; inv_sum 0;
quant_e2 3 1; max_last 1; log_first 0; turn_max 1; log_next 0 0; log_next 0 1; row_max 1; teacher_exp 0 1;
log_next 0 2; ratio_sums 0; log_last 0; factors 0; load_teacher 1 1; load_teacher 1 0;
"""

STEP = """
gain 3 0; gain 3 1; turn_logits 1 1 0; turn_logits 1 0 0; turn_out -1 1 1; logits_mm 2 3; turn_out -1 1 0;
student_exp 1 1 0; diff 0 0; student_exp 1 0 0; turn_logits 1 1 3; turn_h 3 0; logits_out 2 3; copy_h 3 0; diff 0 1;
copy_out -1 1 1; student_exp 1 1 3; turn_logits 1 0 3; logits_mm 2 0; grad 0 0 2; turn_logits 1 1 2; max_tiles 2 3;
student_exp 1 0 3; logits_out 2 0; copy_out -1 1 0; turn_logits 1 0 1; student_exp 1 1 2; logits_mm 2 2;
turn_logits 1 1 1; student_exp 1 0 1; turn_grad 0 0 0; grad 0 1 2; teacher_max 1 0; logits_out 2 2; turn_logits 1 0 2;
copy_grad 0 0 0; max_tiles 2 0; turn_grad 0 0 1; max_tiles 2 2; copy_grad 0 0 1; student_exp 1 1 1; turn_h 3 1;
copy_h 3 1; quant_grad 0 0 2; logits_mm 2 1; student_exp 1 0 2; logits_out 2 1; sum_exp 1; teacher_max 1 1;
turn_grad 0 1 1; root_sum 1; turn_grad 0 1 0; copy_grad 0 1 1; copy_grad 0 1 0; max_groups 2 1; max_tiles 2 1;
out_mm 0 0 0 2; teacher_exp 1 0; quant_out -1 1 0; out_mm 0 0 1 2; out_gain 0 0 0; teacher_exp 1 1; log_first 1;
load_teacher 2 0; quant_grad 0 1 2; log_next 1 0; max_groups 2 0; inv_sum 1; load_teacher 2 1; turn_out 0 0 0;
out_gain 0 0 1; quant_h 3; max_last 2; out_mm 0 1 0 2; log_next 1 1; out_mm 0 1 1 2; turn_out 0 0 1; quant_out -1 1 1;
out_gain 0 1 0; copy_out 0 0 0; log_next 1 2; out_gain 0 1 1; log_last 1; ratio_sums 1; turn_max 2; row_max 2;
copy_out 0 0 1; factors 1; quant_out 0 0 0; quant_out 0 0 1;
"""

LAST = """
diff 3 0; grad 3 0 2; diff 3 1; turn_out 2 1 0; turn_grad 3 0 0; copy_out 2 1 0; turn_grad 3 0 1; copy_grad 3 0 0;
grad 3 1 0; turn_out 2 1 1; copy_grad 3 0 1; quant_grad 3 0 2; grad 3 1 1; turn_grad 3 1 0; copy_out 2 1 1;
copy_grad 3 1 0; quant_grad 3 1 0; out_mm 3 0 0 2; out_mm 3 0 1 2; out_gain 3 0 0; turn_grad 3 1 1; copy_grad 3 1 1;
out_gain 3 0 1; quant_out 2 1 0; turn_out 3 0 0; copy_out 3 0 0; out_mm 3 1 2 0; quant_grad 3 1 1; out_mm 3 1 2 1;
quant_out 2 1 1; out_gain 3 1 0; turn_out 3 0 1; copy_out 3 0 1; quant_out 3 0 0; out_gain 3 1 1; turn_out 3 1 0;
copy_out 3 1 0; turn_out 3 1 1; copy_out 3 1 1; quant_out 3 0 1; quant_out 3 1 0; quant_out 3 1 1;
"""


def entries(table):
    out = []
    for entry in table.replace("\n", " ").split(";"):
        parts = [x for x in entry.split(" ") if x != ""]
        if len(parts) > 0:
            out.append((parts[0], [x if x in ("S", "V") else int(x) for x in parts[1:]]))
    return out


def tile_distillzlosslogitsbackward_x1_kernel(tc, h, gamma, e, a, b, teacher, w, out_0, out_1, out_2):
    nc = tc.nc
    with ExitStack() as ctx:
        sbuf = ctx.enter_context(tc.tile_pool(name="sbuf", bufs=1))
        psum = ctx.enter_context(tc.psum_pool(name="psum", bufs=2))
        ctx.enter_context(tc.manual_schedule())

        buffers = {
            "h": 3,
            "hg": 2,
            "teacher": 2,
            "8k": 7,
            "4k": 9,
            "hg codes": 3,
            "logits": 8,
            "ga codes": 2,
            "out": 4,
            "out4": 2,
            "words": 3,
            "scales": 2,
        }

        def new(shape, dtype, kind, name, bufs=1):
            return sbuf.tile(shape, dtype, name=name, tag=kind, bufs=buffers.get(kind, bufs), align_bytes=64)

        def small(name):
            return new([128, 2], F32, name, name, 2)

        def bank(shape, kind, dtype=F32):
            return psum.tile(shape, dtype, name="bank", tag=kind, bufs=2)

        first = new([128, 1], F32, "first", "first")
        nc.vector.memset(first[:], 0.0)
        nc.scalar.activation(out=first[:], in_=first[:], func=ACT.Exp)
        gamma_in = new([128, D], BF16, "gamma_in", "gamma_in")
        nc.vector.memset(gamma_in[:], 0.0)
        nc.scalar.dma_start(out=gamma_in[0:1, :], in_=gamma.rearrange("(o d) -> o d", o=1))
        ones = new([128, 128], BF16, "ones", "ones")
        nc.vector.memset(ones[:], 1.0)
        vec_in = new([128, 128], BF16, "vec_in", "vec_in")
        nc.vector.memset(vec_in[:], 0.0)
        nc.scalar.dma_start(out=vec_in[0:16, :], in_=a.rearrange("(r c) -> r c", c=128))
        nc.scalar.dma_start(out=vec_in[16:32, :], in_=b.rearrange("(r c) -> r c", c=128))
        nc.scalar.dma_start(out=vec_in[32:40, :], in_=w.rearrange("(r c) -> r c", c=128))
        exponent = new([128, 2], F32, "exponent", "exponent")
        nc.gpsimd.memset(exponent[:], 1.0 / ROOT)
        ident_f = new([128, 128], F32, "ident_f", "ident_f")
        make_identity(nc, ident_f[:])
        ident_b = new([128, 128], BF16, "ident_b", "ident_b")
        make_identity(nc, ident_b[:])

        gamma_row = new([128, D], BF16, "gamma_row", "gamma_row")
        for x in range(2):
            spread = bank([128, 512], "u")
            nc.tensor.matmul(spread[:], lhsT=ones[:], rhs=gamma_in[:, 512 * x : 512 * (x + 1)], start=True, stop=True)
            nc.vector.tensor_copy(out=gamma_row[:, 512 * x : 512 * (x + 1)], in_=spread[:])
        a_row = new([128, V], BF16, "a_row", "a_row")
        cols = new([128, 40], F32, "cols", "cols")
        w_cols = new([128, 8], F32, "w_cols", "w_cols")

        def spread_a():
            nc.sync.dma_start(out=a_row[:], in_=a.partition_broadcast(128))

        def columns():
            turned = bank([128, 128], "logits", BF16)
            nc.tensor.transpose(turned[:], vec_in[:], ident_b[:])
            nc.vector.tensor_copy(out=cols[:], in_=turned[:, 0:40])
            nc.vector.tensor_scalar(out=w_cols[:], in0=cols[:, 32:40], scalar1=LOSS_SCALE, scalar2=None, op0=ALU.mult)

        h_in, t_in, e_in = {}, {}, {}

        def load_h(s, i):
            j = 2 * s + i
            h_in[s, i] = new([128, D], BF16, "h", "h_in")
            nc.sync.dma_start(out=h_in[s, i][:], in_=h[128 * j : 128 * (j + 1), :])

        def load_teacher(s, i):
            j = 2 * s + i
            t_in[s, i] = new([128, V], BF16, "teacher", "t_in")
            nc.sync.dma_start(out=t_in[s, i][:], in_=teacher[128 * j : 128 * (j + 1), :])

        def load_e(g, x, parts):
            if g not in e_in:
                e_in[g] = new([128, 4, D], BF16, "8k", "e_in")
            cs = slice(D // parts * x, D // parts * (x + 1))
            nc.sync.dma_start(out=e_in[g][:, :, cs], in_=e[512 * g : 512 * (g + 1), :].rearrange("(p j) d -> p j d", j=4)[:, :, cs])

        def turn_words(dst, words, base):
            for u in range(2):
                nc.tensor.transpose(dst[:, u, :], words[:, base + u : base + 256 : 2], ident_f[:])

        e1_codes = new([128, 2, V], U32, "e1_codes", "e1_codes")
        e1_scales = new([128, 2, V], U8, "e1_scales", "e1_scales")
        e_turned, e1_bf = {}, {}

        def turn_e(g, f, x):
            words = e_in[g][:].rearrange("p j d -> p (j d)").bitcast(F32)
            e_turned[g, f, x] = bank([128, 2, 2, 128], "turn" if x == 0 else ("out" if f == 0 else "logits"))
            for k in range(2):
                turn_words(e_turned[g, f, x][:, k], words, 512 * (2 * x + k) + 256 * f)

        def copy_e(g, f, x, engine):
            if (g, f) not in e1_bf:
                e1_bf[g, f] = new([128, 512, 4], BF16, "4k", "e1_bf")
            dst = e1_bf[g, f][:].rearrange("q v t -> q (v t)").bitcast(F32).rearrange("q (p x k u) -> q x p k u", x=2, k=2, u=2)
            src = e_turned[g, f, x][:].rearrange("q k u p -> q p k u")
            if engine == "S":
                nc.scalar.copy(out=dst[:, x], in_=src)
            else:
                nc.vector.tensor_copy(out=dst[:, x], in_=src)

        def quant_e1(g, f):
            nc.vector.quantize_mx(
                out=e1_codes[:, f, 512 * g : 512 * (g + 1)].bitcast(FP8X4),
                scales=e1_scales[:, f, 512 * g : 512 * (g + 1)],
                in_=e1_bf[g, f][:].rearrange("q v t -> q (v t)"),
            )

        e2_codes = new([128, 4, D], U32, "e2_codes", "e2_codes")
        e2_scales = new([128, 4, D], U8, "e2_scales", "e2_scales")
        e2_bf = {}

        def interleave_e(g, f, engine):
            e2_bf[g, f] = new([128, 512, 4], BF16, "4k", "e2_bf")
            src = e_in[g][:, :, 512 * f : 512 * (f + 1)]
            if engine == "S":
                nc.scalar.copy(out=e2_bf[g, f][:], in_=src.rearrange("p t c -> p c t"))
            else:
                nc.vector.tensor_copy(out=e2_bf[g, f][:].rearrange("p (c i) t -> p c t i", i=4), in_=src.rearrange("p t (c i) -> p c t i", i=4))

        def quant_e2(g, f):
            nc.vector.quantize_mx(
                out=e2_codes[:, g, 512 * f : 512 * (f + 1)].bitcast(FP8X4),
                scales=e2_scales[:, g, 512 * f : 512 * (f + 1)],
                in_=e2_bf[g, f][:].rearrange("p c t -> p (c t)"),
            )

        hg, hg_turned, hg_bf, hg_codes, hg_scales = {}, {}, {}, {}, {}

        def gain(s, i):
            hg[s, i] = new([128, D], BF16, "hg", "hg")
            nc.vector.tensor_tensor(out=hg[s, i][:], in0=h_in[s, i][:], in1=gamma_row[:], op=ALU.mult)

        def turn_h(s, i):
            hg_turned[s, i] = bank([128, 2, 2, 128], "turn")
            for f in range(2):
                turn_words(hg_turned[s, i][:, f], hg[s, i][:].bitcast(F32), 256 * f)

        def copy_h(s, i):
            if s not in hg_bf:
                hg_bf[s] = new([128, 2, 256, 4], BF16, "4k", "hg_bf")
            dst = hg_bf[s][:].rearrange("q f n t -> q (f n t)").bitcast(F32).rearrange("q (f i n u) -> q i f n u", f=2, i=2, u=2)
            nc.scalar.copy(out=dst[:, i], in_=hg_turned[s, i][:].rearrange("q f u n -> q f n u"))

        def quant_h(s):
            hg_codes[s] = new([128, 2, 256], U32, "hg codes", "hg_codes")
            hg_scales[s] = new([128, 2, 256], U8, "hg scales", "hg_scales", 3)
            nc.vector.quantize_mx(
                out=hg_codes[s][:].rearrange("q f n -> q (f n)").bitcast(FP8X4),
                scales=hg_scales[s][:].rearrange("q f n -> q (f n)"),
                in_=hg_bf[s][:].rearrange("q f n t -> q (f n t)"),
            )

        u_banks, logits = {}, {}

        def logits_mm(s, g):
            for k in range(4):
                if k % 2 == 0:
                    u_banks[s, g, k // 2] = bank([128, 2, 256], "u")
                j = 4 * g + k
                for f in range(2):
                    nc.tensor.matmul_mx(
                        out=u_banks[s, g, k // 2][:, k % 2, :],
                        lhsT=e1_codes[:, f, 128 * j : 128 * (j + 1)].bitcast(FP8X4),
                        lhsT_scale=e1_scales[:, f, 128 * j : 128 * (j + 1)],
                        rhs=hg_codes[s][:, f, :].bitcast(FP8X4),
                        rhs_scale=hg_scales[s][:, f, :],
                        start=(f == 0),
                        stop=(f == 1),
                    )

        def logits_out(s, g):
            logits[s, g] = new([128, 4, 256], F32, "logits", "logits")
            for k in range(4):
                j = 4 * g + k
                nc.scalar.activation(out=logits[s, g][:, k, :], in_=u_banks[s, g, k // 2][:, k % 2, :], func=ACT.Identity, bias=cols[:, 16 + j : 17 + j], scale=cols[:, j : j + 1])

        max_a, max_b, max_c, max_turned, neg_max = {}, {}, {}, {}, {}

        def max_tiles(s, g):
            if (s, g // 2) not in max_a:
                max_a[s, g // 2] = new([128, 2, 512], BF16, "max_a", "max_a", 2)
            nc.vector.tensor_tensor(out=max_a[s, g // 2][:, g % 2, :].rearrange("p (k n) -> p k n", k=2), in0=logits[s, g][:, 0:2, :], in1=logits[s, g][:, 2:4, :], op=ALU.max)

        def max_groups(s, x):
            if s not in max_b:
                max_b[s] = new([128, 2, 512], BF16, "max_b", "max_b", 2)
            nc.vector.tensor_tensor(out=max_b[s][:, x, :], in0=max_a[s, x][:, 0, :], in1=max_a[s, x][:, 1, :], op=ALU.max)

        def max_last(s):
            half = new([128, 512], BF16, "half", "half")
            nc.vector.tensor_tensor(out=half[:], in0=max_b[s][:, 0, :], in1=max_b[s][:, 1, :], op=ALU.max)
            max_c[s] = new([128, 256], BF16, "max_c", "max_c", 2)
            nc.vector.tensor_tensor(out=max_c[s][:], in0=half[:, 0:256], in1=half[:, 256:512], op=ALU.max)

        def turn_max(s):
            max_turned[s] = bank([128, 2, 128], "turn", BF16)
            for i in range(2):
                nc.tensor.transpose(max_turned[s][:, i, :], max_c[s][:, 128 * i : 128 * (i + 1)], ident_b[:])

        def row_max(s):
            neg_max[s] = small("neg_max")
            nc.vector.tensor_reduce(out=neg_max[s][:], in_=max_turned[s][:], axis=AX.X, op=ALU.max, negate=True)

        t_shift, t_sum, t_exp = {}, {}, {}

        def teacher_max(s, i):
            if s not in t_shift:
                t_shift[s] = small("t_shift")
            t = t_in[s, i]
            nc.vector.tensor_scalar(out=t[:], in0=t[:], scalar1=-0.5, scalar2=None, op0=ALU.mult, op1=ALU.min, accum_out=t_shift[s][:, i : i + 1])

        def teacher_exp(s, i):
            if s not in t_sum:
                t_sum[s] = small("t_sum")
            t_exp[s, i] = new([128, V], F32, "8k", "t_exp")
            nc.scalar.activation(out=t_exp[s, i][:], in_=t_in[s, i][:], func=ACT.Exp, bias=t_shift[s][:, i : i + 1], scale=-1.0, accum_out=t_sum[s][:, i : i + 1])

        turned, p_exp, part_sums = {}, {}, {}

        def turn_logits(s, i, g):
            turned[s, i, g] = bank([128, 4, 128], "logits")
            for k in range(4):
                nc.tensor.transpose(turned[s, i, g][:, k, :], logits[s, g][:, k, 128 * i : 128 * (i + 1)], ident_f[:])

        def student_exp(s, i, g):
            if (s, i) not in p_exp:
                p_exp[s, i] = new([128, V], F32, "8k", "p_exp")
            if s not in part_sums:
                part_sums[s] = new([128, 2, 4], F32, "part_sums", "part_sums", 2)
            nc.scalar.activation(
                out=p_exp[s, i][:, 512 * g : 512 * (g + 1)],
                in_=turned[s, i, g][:].rearrange("p k v -> p (k v)"),
                func=ACT.Exp,
                bias=neg_max[s][:, i : i + 1],
                scale=1.0,
                accum_out=part_sums[s][:, i, g : g + 1],
            )

        p_sum, p_inv, z, d_z, series, lse, t_inv, ratio, p_factor, row_factor = {}, {}, {}, {}, {}, {}, {}, {}, {}, {}

        def sum_exp(s):
            p_sum[s] = small("p_sum")
            nc.vector.tensor_reduce(out=p_sum[s][:], in_=part_sums[s][:], axis=AX.X, op=ALU.add)

        def root_sum(s):
            z[s] = small("z")
            nc.gpsimd.tensor_tensor(out=z[s][:], in0=p_sum[s][:], in1=exponent[:], op=ALU.pow)

        def inv_sum(s):
            p_inv[s] = small("p_inv")
            nc.vector.reciprocal(out=p_inv[s][:], in_=p_sum[s][:])

        def log_first(s):
            d_z[s] = small("d_z")
            nc.vector.tensor_scalar(out=d_z[s][:], in0=z[s][:], scalar1=1.0, scalar2=None, op0=ALU.subtract)
            series[s, 0] = small("series0")
            nc.vector.tensor_scalar(out=series[s, 0][:], in0=z[s][:], scalar1=1.0, scalar2=-0.25, op0=ALU.subtract, op1=ALU.mult)

        def log_next(s, k):
            series[s, k + 1] = small("series%d" % (k + 1))
            nc.vector.scalar_tensor_tensor(out=series[s, k + 1][:], in0=series[s, k][:], scalar=(1.0 / 3.0, -0.5, 1.0)[k], in1=d_z[s][:], op0=ALU.add, op1=ALU.mult)

        def log_last(s):
            lse[s] = small("lse")
            nc.vector.scalar_tensor_tensor(out=lse[s][:], in0=series[s, 3][:], scalar=ROOT, in1=neg_max[s][:], op0=ALU.mult, op1=ALU.subtract)

        def ratio_sums(s):
            t_inv[s] = small("t_inv")
            nc.vector.reciprocal(out=t_inv[s][:], in_=t_sum[s][:])
            ratio[s] = small("ratio")
            nc.vector.scalar_tensor_tensor(out=ratio[s][:], in0=t_sum[s][:], scalar=Z_COEF, in1=p_inv[s][:], op0=ALU.mult, op1=ALU.mult)

        def factors(s):
            row_factor[s] = small("row_factor")
            nc.vector.tensor_tensor(out=row_factor[s][:], in0=t_inv[s][:], in1=w_cols[:, 2 * s : 2 * s + 2], op=ALU.mult)
            p_factor[s] = small("p_factor")
            nc.vector.scalar_tensor_tensor(out=p_factor[s][:], in0=lse[s][:], scalar=1.0 / Z_COEF, in1=ratio[s][:], op0=ALU.add, op1=ALU.mult)

        ga, ga_turned, ga_bf, ga_codes, ga_scales = {}, {}, {}, {}, {}

        def halves(part):
            return (0, 1) if part == 2 else (part,)

        def groups(part):
            return (0, 4) if part == 2 else (2 * part, 2 * part + 2)

        def diff(s, i):
            nc.vector.scalar_tensor_tensor(out=p_exp[s, i][:], in0=p_exp[s, i][:], scalar=p_factor[s][:, i : i + 1], in1=t_exp[s, i][:], op0=ALU.mult, op1=ALU.subtract)

        def grad(s, i, part):
            if (s, i) not in ga:
                ga[s, i] = new([128, V], BF16, "4k", "ga")
            g0, g1 = groups(part)
            cs = slice(512 * g0, 512 * g1)
            nc.vector.scalar_tensor_tensor(out=ga[s, i][:, cs], in0=p_exp[s, i][:, cs], scalar=row_factor[s][:, i : i + 1], in1=a_row[:, cs], op0=ALU.mult, op1=ALU.mult)

        def turn_grad(s, i, x):
            ga_turned[s, i, x] = bank([128, 2, 2, 128], "turn")
            for k in range(2):
                turn_words(ga_turned[s, i, x][:, k], ga[s, i][:].bitcast(F32), 256 * (2 * x + k))

        def copy_grad(s, i, x):
            if (s, i) not in ga_bf:
                ga_bf[s, i] = new([128, 4, 128, 4], BF16, "4k", "ga_bf")
            dst = ga_bf[s, i][:].rearrange("q g n t -> q (g n t)").bitcast(F32).rearrange("q (x k n u) -> q x k n u", x=2, k=2, u=2)
            nc.scalar.copy(out=dst[:, x], in_=ga_turned[s, i, x][:].rearrange("q k u n -> q k n u"))

        def quant_grad(s, i, part):
            if (s, i) not in ga_codes:
                ga_codes[s, i] = new([128, 512], U32, "ga codes", "ga_codes")
                ga_scales[s, i] = new([128, 512], U8, "ga scales", "ga_scales", 2)
            g0, g1 = groups(part)
            nc.vector.quantize_mx(
                out=ga_codes[s, i][:, 128 * g0 : 128 * g1].bitcast(FP8X4),
                scales=ga_scales[s, i][:, 128 * g0 : 128 * g1],
                in_=ga_bf[s, i][:, g0:g1].rearrange("q g n t -> q (g n t)"),
            )

        out_banks, out_sb, out_turned, out_bf, words_out, scales_out = {}, {}, {}, {}, {}, {}

        def out_mm(s, i, f, part):
            g0, g1 = groups(part)
            for x in halves(f):
                if (s, i, x) not in out_banks:
                    out_banks[s, i, x] = bank([128, 512], "out")
                for g in range(g0, g1):
                    nc.tensor.matmul_mx(
                        out=out_banks[s, i, x][:],
                        lhsT=ga_codes[s, i][:, 128 * g : 128 * (g + 1)].bitcast(FP8X4),
                        lhsT_scale=ga_scales[s, i][:, 128 * g : 128 * (g + 1)],
                        rhs=e2_codes[:, g, 512 * x : 512 * (x + 1)].bitcast(FP8X4),
                        rhs_scale=e2_scales[:, g, 512 * x : 512 * (x + 1)],
                        start=(g == 0),
                        stop=(g == 3),
                    )

        def out_gain(s, i, f):
            out_sb[s, i, f] = new([128, 512], F32, "out", "out_sb")
            nc.vector.tensor_tensor(out=out_sb[s, i, f][:], in0=out_banks[s, i, f][:], in1=gamma_row[:, 512 * f : 512 * (f + 1)], op=ALU.mult)
            n0 = 128 * (2 * s + i)
            nc.sync.dma_start(out=out_0[n0 : n0 + 128, 512 * f : 512 * (f + 1)], in_=out_sb[s, i, f][:])

        def turn_out(s, i, f):
            out_turned[s, i, f] = bank([128, 4, 128], "turn")
            for t in range(4):
                nc.tensor.transpose(out_turned[s, i, f][:, t, :], out_sb[s, i, f][:, t:512:4], ident_f[:])

        def copy_out(s, i, f):
            if (s, i) not in out_bf:
                out_bf[s, i] = new([128, 2, 128, 4], BF16, "out4", "out_bf")
            nc.scalar.copy(out=out_bf[s, i][:, f], in_=out_turned[s, i, f][:].rearrange("q t n -> q n t"))

        words_hbm = out_1.bitcast(I32).rearrange("g p m o -> p g (m o)")
        scales_hbm = out_2.bitcast(I32).rearrange("g q m -> q g m")

        def quant_out(s, i, f):
            if s not in scales_out:
                scales_out[s] = new([128, 2, 256], U8, "scales", "scales_out")
            if (s, i) not in words_out:
                words_out[s, i] = new([128, 2, 128], U32, "words", "words_out")
            nc.vector.quantize_mx(
                out=words_out[s, i][:, f, :].bitcast(FP8X4),
                scales=scales_out[s][:, f, 128 * i : 128 * (i + 1)],
                in_=out_bf[s, i][:, f].rearrange("q n t -> q (n t)"),
            )
            n0 = 128 * (2 * s + i)
            if f == 1:
                nc.sync.dma_start(out=words_hbm[:, :, n0 : n0 + 128], in_=words_out[s, i][:].bitcast(I32))
            if i == 1 and f == 1:
                live = scales_out[s][:].bitcast(I32)
                for Q in range(4):
                    nc.sync.dma_start(out=scales_hbm[4 * Q : 4 * Q + 4, :, 64 * s : 64 * (s + 1)], in_=live[32 * Q : 32 * Q + 4, :, :])

        helpers = dict(
            load_h=load_h, load_teacher=load_teacher, load_e=load_e, spread_a=spread_a, columns=columns,
            turn_e=turn_e, copy_e=copy_e, quant_e1=quant_e1, interleave_e=interleave_e, quant_e2=quant_e2,
            gain=gain, turn_h=turn_h, copy_h=copy_h, quant_h=quant_h, logits_mm=logits_mm, logits_out=logits_out,
            max_tiles=max_tiles, max_groups=max_groups, max_last=max_last, turn_max=turn_max, row_max=row_max,
            teacher_max=teacher_max, teacher_exp=teacher_exp, turn_logits=turn_logits, student_exp=student_exp,
            sum_exp=sum_exp, root_sum=root_sum, inv_sum=inv_sum, log_first=log_first, log_next=log_next, log_last=log_last,
            ratio_sums=ratio_sums, factors=factors, diff=diff, grad=grad, turn_grad=turn_grad, copy_grad=copy_grad,
            quant_grad=quant_grad, out_mm=out_mm, out_gain=out_gain, turn_out=turn_out, copy_out=copy_out, quant_out=quant_out,
        )
        for name, args in entries(FIRST):
            helpers[name](*args)
        for s in range(3):
            for name, args in entries(STEP):
                if 0 <= s + args[0] < 4:
                    helpers[name](s + args[0], *args[1:])
        for name, args in entries(LAST):
            helpers[name](*args)
